import numpy as np
import ml_dtypes


def mxq(x, axis, fmt="e4m3"):
    dtype, down = {"e4m3": (ml_dtypes.float8_e4m3fn, 7), "e5m2": (ml_dtypes.float8_e5m2, 14)}[fmt]
    v = np.moveaxis(np.asarray(x, np.float32).astype(ml_dtypes.bfloat16).astype(np.float64), axis, -1)
    blocks = v.reshape(v.shape[:-1] + (-1, 32))
    amax = np.abs(blocks).max(-1, keepdims=True)
    byte = np.maximum(np.where(amax > 0, np.frexp(amax)[1] - 1 + 127, 0) - down, 1)
    scale = np.exp2(byte - 127.0)
    codes = (blocks / scale).astype(np.float32).astype(dtype).astype(np.float64)
    return np.moveaxis((codes * scale).reshape(v.shape), -1, axis)


WIDE = False


def mx_kscale(k):
    if not WIDE:
        return np.ones(k)
    levels = np.array([10, -10, 5, -5, 0])
    if k % 512:
        return np.exp2(np.random.permutation(np.resize(levels, k // 32))).repeat(32)
    a = np.empty((k // 512, 16))
    for p in range(k // 512):
        a[p, :8] = np.random.permutation(np.resize(levels, 8))
        for g in range(8):
            far = levels[np.abs(levels - a[p, g]) >= 10]
            a[p, g + 8] = far[np.random.randint(len(far))]
    return np.exp2(a.ravel()).repeat(32)


def f64(x):
    return np.asarray(x).astype(np.float64)


def striped(idx):
    return np.tile(idx.reshape(-1, 16).T, (8, 1)).astype(np.uint16)


def unstriped(offs):
    return offs[:16].T.reshape(-1).astype(np.int64)


def pack_weight(w):
    k, n = w.shape
    w = f64(np.asarray(w, np.float32).astype(ml_dtypes.bfloat16)).reshape(k // 32, 32, n)
    amax = np.abs(w).max(1)
    byte = np.clip(np.where(amax > 0, np.frexp(amax)[1] - 1 + 127 - 7, 1), 1, 254)
    scaled = (w * np.exp2(127.0 - byte)[:, None, :]).reshape(k, n).astype(np.float32)
    words = np.ascontiguousarray(scaled.reshape(k // 512, 128, 4, n).transpose(0, 1, 3, 2)).astype(ml_dtypes.float8_e4m3fn).view(np.uint8)
    return words, np.ascontiguousarray(byte.astype(np.uint8).reshape(k // 512, 16, n))


def unpack_weight(words, scales):
    g, p, n, _ = words.shape
    vals = np.ascontiguousarray(words).view(ml_dtypes.float8_e4m3fn).astype(np.float64) * np.repeat(np.exp2(scales.astype(np.float64) - 127.0), 8, axis=1)[..., None]
    return vals.transpose(0, 1, 3, 2).reshape(g * 512, n)


K, T, S, V, N, D = 1024, 2048, 512, 256, 256, 4
P = 2 ** 7


def setup_inputs():
    n = np.random.standard_normal
    s = mx_kscale(K)[:, None]
    near = np.random.permutation(S)
    packed_xT = pack_weight(n((K, T)) * s)
    return {
        "x_words": packed_xT[0],
        "x_scales": packed_xT[1],
        "w1": (n((K, N)) / np.sqrt(K) / s).astype(np.float32),
        "op": (np.tile(np.random.uniform(0.2, 0.95, S), (P, 1))).astype(np.float32),
        "fall": (np.tile(np.random.uniform(0.2, 1.0, (D, 1, V)), (1, P, 1))).astype(np.float32),
        "offs": striped(np.random.permutation(T)[:S]),
        "pos1": striped(near[:V]),
        "pos2": striped(near[V:]),
        "pos3": striped(np.random.permutation(S)[:V]),
        "pos4": striped(np.random.permutation(S)[:V]),
    }


def reference(x_words, x_scales, w1, op, fall, offs, pos1, pos2, pos3, pos4):
    xq = unpack_weight(x_words, x_scales)[:, unstriped(offs)]
    h = mxq(f64(w1), 0, "e4m3").T @ xq
    a0 = (f64(op)[:1][:, unstriped(pos1)]) * f64(fall)[0, :1]
    a1 = (f64(op)[:1][:, unstriped(pos2)]) * f64(fall)[1, :1]
    t0 = -1.0 * a0 + 1.0
    c1 = a1 * t0
    a2 = (f64(op)[:1][:, unstriped(pos3)]) * f64(fall)[2, :1]
    t1 = t0 - (t0 * a1)
    c2 = a2 * t1
    a3 = (f64(op)[:1][:, unstriped(pos4)]) * f64(fall)[3, :1]
    t2 = t1 - (t1 * a2)
    c3 = a3 * t2
    return h[:, unstriped(pos1)] * a0 + h[:, unstriped(pos2)] * c1 + h[:, unstriped(pos3)] * c2 + h[:, unstriped(pos4)] * c3

@@ -1,0 +1,191 @@
+from contextlib import ExitStack
+
+import concourse.mybir as mybir
+from concourse.masks import make_identity
+
+K, T, S, V, N, D = 1024, 2048, 512, 256, 256, 4
+P = 128
+PACK = 4
+PASSES = K // (P * PACK)
+M_TILES = N // P
+V_BLOCKS = V // P
+HALF = S // 2
+ROWS = 32
+
+FLOPS = 2 * K * N * S
+
+F32 = mybir.dt.float32
+BF16 = mybir.dt.bfloat16
+I32 = mybir.dt.int32
+U32 = mybir.dt.uint32
+U16 = mybir.dt.uint16
+U8 = mybir.dt.uint8
+FP8X4 = mybir.dt.float8_e4m3fn_x4
+COPY = mybir.ActivationFunctionType.Copy
+IDENTITY = mybir.ActivationFunctionType.Identity
+MULT = mybir.AluOpType.mult
+ADD = mybir.AluOpType.add
+
+
+def tile_picked_ysplat_none_p_kernel(
+    tc, x_words, x_scales, w1, op, fall, offs, pos1, pos2, pos3, pos4, out
+):
+    nc = tc.nc
+    with ExitStack() as ctx:
+        held = ctx.enter_context(tc.tile_pool(name="held", bufs=1))
+        ring = ctx.enter_context(tc.tile_pool(name="ring", bufs=3))
+        psum = ctx.enter_context(tc.psum_pool(name="psum", bufs=1))
+
+        def bank(index):
+            return psum.tile([P, 512], F32, name="bank%d" % index)
+
+        offs_t = held.tile([P, S // 16], U16, name="offs_t")
+        pos_t = [held.tile([P, V // 16], U16, name="pos_t%d" % d) for d in range(D)]
+        op_t = held.tile([P, S], F32, name="op_t")
+        fall_t = held.tile([P, V], F32, name="fall_t")
+        words = [held.tile([P, T], I32, name="words%d" % o) for o in range(PASSES)]
+        scales = held.tile([P, T], U8, name="scales")
+        w_raw = [held.tile([P, PACK, N], F32, name="w_raw%d" % o) for o in range(PASSES)]
+        ident = held.tile([P, P], F32, name="ident")
+
+        nc.vector.memset(scales[:].bitcast(I32), 0)
+        for t in (op_t, fall_t):
+            nc.vector.memset(t[32:64, :], 0.0)
+            nc.vector.memset(t[64:128, :], 0.0)
+        make_identity(nc, ident[:])
+
+        def load_words(o):
+            nc.sync.dma_start(words[o][:], x_words[o].rearrange("p c r -> p (c r)").bitcast(I32))
+
+        def load_w(o):
+            rows = w1[o * 512 : (o + 1) * 512, :]
+            nc.sync.dma_start(w_raw[o][:], rows.rearrange("(p j) n -> p j n", j=PACK))
+
+        nc.sync.dma_start(op_t[0:ROWS, :], op[0:ROWS, :])
+        for d, pos in enumerate((pos1, pos2, pos3, pos4)):
+            nc.sync.dma_start(pos_t[d][:], pos)
+        nc.sync.dma_start(offs_t[:], offs)
+        load_words(0)
+        load_w(0)
+        nc.sync.dma_start(fall_t[0:ROWS, :], fall[:, 0 : ROWS // D, :])
+        for q in range(4):
+            nc.sync.dma_start(
+                scales[32 * q : 32 * q + 4 * PASSES, :].bitcast(I32),
+                x_scales[:, 4 * q : 4 * q + 4, :].bitcast(I32),
+            )
+        load_w(1)
+        load_words(1)
+
+        def turn(dst_bank, src):
+            for b in range(V_BLOCKS):
+                nc.tensor.transpose(dst_bank[:, b * P : (b + 1) * P], src[:, b * P : (b + 1) * P], ident[:])
+
+        fall_bank = bank(0)
+        turn(fall_bank, fall_t)
+        fall_col = held.tile([P, V_BLOCKS, D], F32, name="fall_col")
+        nc.scalar.activation(
+            fall_col[:],
+            fall_bank[:, 0:V].rearrange("p (b r) -> p b r", b=V_BLOCKS)[:, :, 0 : ROWS : ROWS // D],
+            COPY,
+        )
+
+        def look_up_op(d):
+            picked = held.tile([P, V], F32, name="op_picked%d" % d)
+            nc.vector.tensor_copy(picked[:], op_t[:].indirect(pos_t[d][:]))
+            turned = bank(1 + d)
+            turn(turned, picked)
+            return turned
+
+        pair = held.tile([P, V_BLOCKS, D, 2], F32, name="pair")
+        for d in range(D):
+            turned = look_up_op(d)
+            for b in range(V_BLOCKS):
+                nc.scalar.activation(pair[:, b, d, 0:1], turned[:, b * P : b * P + 1], COPY, scale=fall_col[:, b, d : d + 1])
+        nc.scalar.activation(pair[:, :, 0 : D - 1, 1], pair[:, :, 0 : D - 1, 0], IDENTITY, scale=-1.0, bias=1.0)
+
+        a0_bank = bank(5)
+        for b in range(V_BLOCKS):
+            nc.tensor.transpose(a0_bank[:, b * P : (b + 1) * P], pair[:, b, 0, 0:1].to_broadcast([P, P]), ident[:])
+        a0_rows = held.tile([P, V], F32, name="a0_rows")
+        nc.scalar.copy(a0_rows[:], a0_bank[:, 0:V])
+
+        ct = held.tile([P, V_BLOCKS, D, 2], F32, name="ct")
+        for b in range(V_BLOCKS):
+            nc.scalar.activation(ct[:, b, 1, :], pair[:, b, 1, :], COPY, scale=pair[:, b, 0, 1:2])
+        for b in range(V_BLOCKS):
+            nc.scalar.activation(ct[:, b, 2, :], pair[:, b, 2, :], COPY, scale=ct[:, b, 1, 1:2])
+        for b in range(V_BLOCKS):
+            nc.scalar.activation(ct[:, b, 3, 0:1], pair[:, b, 3, 0:1], COPY, scale=ct[:, b, 2, 1:2])
+
+        x_codes = [held.tile([P, S], U32, name="x_codes%d" % o, align_bytes=64) for o in range(PASSES)]
+        x_planes = held.tile([P, S], U8, name="x_planes", align_bytes=64)
+        w_codes = [held.tile([P, N], U32, name="w_codes%d" % o, align_bytes=64) for o in range(PASSES)]
+        w_planes = [held.tile([P, N], U8, name="w_planes%d" % o, align_bytes=64) for o in range(PASSES)]
+
+        def quantise_w(o):
+            grouped = held.tile([P, N, PACK], BF16, name="grouped%d" % o, align_bytes=64)
+            nc.scalar.activation(
+                grouped[:].rearrange("p (c i) j -> p c j i", i=4),
+                w_raw[o][:].rearrange("p j (c i) -> p c j i", i=4),
+                COPY,
+            )
+            nc.vector.quantize_mx(
+                out=w_codes[o][:].bitcast(FP8X4),
+                scales=w_planes[o][:],
+                in_=grouped[:].rearrange("p n j -> p (n j)"),
+            )
+
+        def product_pass(acc, m, o, cols):
+            nc.tensor.matmul_mx(
+                out=acc,
+                lhsT=w_codes[o][:, m * P : (m + 1) * P].bitcast(FP8X4),
+                lhsT_scale=w_planes[o][:, m * P : (m + 1) * P],
+                rhs=x_codes[o][:, cols].bitcast(FP8X4),
+                rhs_scale=x_planes[4 * o : P, cols],
+                start=(o == 0),
+                stop=(o == PASSES - 1),
+            )
+
+        nc.vector.tensor_copy(x_codes[0][:], words[0][:].bitcast(U32).indirect(offs_t[:]))
+        quantise_w(0)
+        nc.vector.tensor_copy(x_planes[:], scales[:].indirect(offs_t[:]))
+        quantise_w(1)
+        h = [held.tile([P, S], F32, name="h%d" % m) for m in range(M_TILES)]
+        halves = [slice(0, HALF), slice(HALF, S)]
+        h0_banks = [bank(6), bank(7)]
+        h1_bank = bank(0)
+        for i in range(2):
+            product_pass(h0_banks[i][:, 0:HALF], 0, 0, halves[i])
+        product_pass(h1_bank[:], 1, 0, slice(0, S))
+        for i in range(2):
+            nc.vector.tensor_copy(
+                x_codes[1][:, halves[i]], words[1][:].bitcast(U32).indirect(offs_t[:, i * HALF // 16 : (i + 1) * HALF // 16])
+            )
+            product_pass(h0_banks[i][:, 0:HALF], 0, 1, halves[i])
+            nc.scalar.copy(h[0][:, halves[i]], h0_banks[i][:, 0:HALF])
+        product_pass(h1_bank[:], 1, 1, slice(0, S))
+        nc.scalar.copy(h[1][:], h1_bank[:])
+
+        total = [bank(5 + m) for m in range(M_TILES)]
+        for m in range(M_TILES):
+            for d in range(1, D):
+                picked = ring.tile([P, V], F32, name="picked")
+                nc.vector.tensor_copy(picked[:], h[m][:].indirect(pos_t[d][:]))
+                turned = bank(d)
+                turn(turned, picked)
+                weighted = ring.tile([P, V], F32, name="weighted")
+                for b in range(V_BLOCKS):
+                    cols = slice(b * P, (b + 1) * P)
+                    nc.scalar.activation(weighted[:, cols], turned[:, cols], COPY, scale=ct[:, b, d, 0:1])
+                for b in range(V_BLOCKS):
+                    cols = slice(b * P, (b + 1) * P)
+                    nc.tensor.matmul(
+                        total[m][:, cols], weighted[:, cols], ident[:], is_transpose=True,
+                        start=(d == 1 and b == 0), stop=(d == D - 1 and b == V_BLOCKS - 1),
+                    )
+        for m in range(M_TILES):
+            picked = ring.tile([P, V], F32, name="picked")
+            nc.vector.tensor_tensor(picked[:], h[m][:].indirect(pos_t[0][:]), a0_rows[:], MULT)
+            result = ring.tile([P, V], F32, name="result")
+            nc.vector.tensor_tensor(result[:], total[m][:, 0:V], picked[:], ADD)
+            nc.sync.dma_start(out[m * P : (m + 1) * P, :], result[:])

@@ -22,7 +22,6 @@ U16 = mybir.dt.uint16
 U8 = mybir.dt.uint8
 FP8X4 = mybir.dt.float8_e4m3fn_x4
 COPY = mybir.ActivationFunctionType.Copy
-IDENTITY = mybir.ActivationFunctionType.Identity
 MULT = mybir.AluOpType.mult
 ADD = mybir.AluOpType.add
 
@@ -45,14 +44,15 @@ def tile_picked_ysplat_none_p_kernel(
         fall_t = held.tile([P, V], F32, name="fall_t")
         words = [held.tile([P, T], I32, name="words%d" % o) for o in range(PASSES)]
         scales = held.tile([P, T], U8, name="scales")
-        w_raw = [held.tile([P, PACK, N], F32, name="w_raw%d" % o) for o in range(PASSES)]
+        w_raw = [held.tile([P, PACK, N], F32, name="w_raw%d" % o, tag="raw%d" % o) for o in range(PASSES)]
         ident = held.tile([P, P], F32, name="ident")
 
-        nc.vector.memset(scales[:].bitcast(I32), 0)
-        for t in (op_t, fall_t):
-            nc.vector.memset(t[32:64, :], 0.0)
-            nc.vector.memset(t[64:128, :], 0.0)
+        nc.gpsimd.memset(scales[:].bitcast(I32), 0)
         make_identity(nc, ident[:])
+        nc.vector.memset(op_t[32:64, :], 0.0)
+        nc.vector.memset(op_t[64:128, :], 0.0)
+        nc.vector.memset(fall_t[0:64, :], 0.0)
+        nc.vector.memset(fall_t[96:128, :], 0.0)
 
         def load_words(o):
             nc.sync.dma_start(words[o][:], x_words[o].rearrange("p c r -> p (c r)").bitcast(I32))
@@ -61,13 +61,16 @@ def tile_picked_ysplat_none_p_kernel(
             rows = w1[o * 512 : (o + 1) * 512, :]
             nc.sync.dma_start(w_raw[o][:], rows.rearrange("(p j) n -> p j n", j=PACK))
 
+        fall_rows = fall.rearrange("d p v -> (d p) v")
         nc.sync.dma_start(op_t[0:ROWS, :], op[0:ROWS, :])
-        for d, pos in enumerate((pos1, pos2, pos3, pos4)):
-            nc.sync.dma_start(pos_t[d][:], pos)
+        nc.sync.dma_start(pos_t[0][:], pos1)
+        nc.sync.dma_start(fall_t[64 : 64 + ROWS, :], fall_rows[0 : D * P : D * P // ROWS, :])
+        nc.sync.dma_start(pos_t[1][:], pos2)
+        nc.sync.dma_start(pos_t[2][:], pos3)
         nc.sync.dma_start(offs_t[:], offs)
         load_words(0)
         load_w(0)
-        nc.sync.dma_start(fall_t[0:ROWS, :], fall[:, 0 : ROWS // D, :])
+        nc.sync.dma_start(pos_t[3][:], pos4)
         for q in range(4):
             nc.sync.dma_start(
                 scales[32 * q : 32 * q + 4 * PASSES, :].bitcast(I32),
@@ -85,45 +88,35 @@ def tile_picked_ysplat_none_p_kernel(
         fall_col = held.tile([P, V_BLOCKS, D], F32, name="fall_col")
         nc.scalar.activation(
             fall_col[:],
-            fall_bank[:, 0:V].rearrange("p (b r) -> p b r", b=V_BLOCKS)[:, :, 0 : ROWS : ROWS // D],
+            fall_bank[:, 0:V].rearrange("p (b r) -> p b r", b=V_BLOCKS)[:, :, 64 : 64 + ROWS : ROWS // D],
             COPY,
         )
 
-        def look_up_op(d):
+        op_col = held.tile([P, V_BLOCKS, D - 1], F32, name="op_col")
+
+        def look_up_op(d, column):
             picked = held.tile([P, V], F32, name="op_picked%d" % d)
             nc.vector.tensor_copy(picked[:], op_t[:].indirect(pos_t[d][:]))
             turned = bank(1 + d)
             turn(turned, picked)
-            return turned
+            nc.scalar.copy(column, turned[:, 0:V:P])
 
         pair = held.tile([P, V_BLOCKS, D, 2], F32, name="pair")
-        for d in range(D):
-            turned = look_up_op(d)
-            for b in range(V_BLOCKS):
-                nc.scalar.activation(pair[:, b, d, 0:1], turned[:, b * P : b * P + 1], COPY, scale=fall_col[:, b, d : d + 1])
-        nc.scalar.activation(pair[:, :, 0 : D - 1, 1], pair[:, :, 0 : D - 1, 0], IDENTITY, scale=-1.0, bias=1.0)
-
-        a0_bank = bank(5)
-        for b in range(V_BLOCKS):
-            nc.tensor.transpose(a0_bank[:, b * P : (b + 1) * P], pair[:, b, 0, 0:1].to_broadcast([P, P]), ident[:])
-        a0_rows = held.tile([P, V], F32, name="a0_rows")
-        nc.scalar.copy(a0_rows[:], a0_bank[:, 0:V])
-
         ct = held.tile([P, V_BLOCKS, D, 2], F32, name="ct")
-        for b in range(V_BLOCKS):
-            nc.scalar.activation(ct[:, b, 1, :], pair[:, b, 1, :], COPY, scale=pair[:, b, 0, 1:2])
-        for b in range(V_BLOCKS):
-            nc.scalar.activation(ct[:, b, 2, :], pair[:, b, 2, :], COPY, scale=ct[:, b, 1, 1:2])
-        for b in range(V_BLOCKS):
-            nc.scalar.activation(ct[:, b, 3, 0:1], pair[:, b, 3, 0:1], COPY, scale=ct[:, b, 2, 1:2])
+        for d in range(D - 1):
+            look_up_op(d, op_col[:, :, d])
+        nc.gpsimd.tensor_tensor(pair[:, :, 0 : D - 1, 0], op_col[:], fall_col[:, :, 0 : D - 1], MULT)
+        nc.gpsimd.tensor_scalar(pair[:, :, 0 : D - 1, 1], pair[:, :, 0 : D - 1, 0], -1.0, 1.0, MULT, ADD)
+        nc.gpsimd.tensor_tensor(ct[:, :, 1, :], pair[:, :, 1, :], pair[:, :, 0, 1:2].to_broadcast([P, V_BLOCKS, 2]), MULT)
+        nc.gpsimd.tensor_tensor(ct[:, :, 2, :], pair[:, :, 2, :], ct[:, :, 1, 1:2].to_broadcast([P, V_BLOCKS, 2]), MULT)
 
-        x_codes = [held.tile([P, S], U32, name="x_codes%d" % o, align_bytes=64) for o in range(PASSES)]
+        x_codes = [held.tile([P, S], U32, name="x_codes0", align_bytes=64)]
         x_planes = held.tile([P, S], U8, name="x_planes", align_bytes=64)
         w_codes = [held.tile([P, N], U32, name="w_codes%d" % o, align_bytes=64) for o in range(PASSES)]
         w_planes = [held.tile([P, N], U8, name="w_planes%d" % o, align_bytes=64) for o in range(PASSES)]
 
         def quantise_w(o):
-            grouped = held.tile([P, N, PACK], BF16, name="grouped%d" % o, align_bytes=64)
+            grouped = held.tile([P, N, PACK], BF16, name="grouped%d" % o, tag="stage%d" % o, align_bytes=64)
             nc.scalar.activation(
                 grouped[:].rearrange("p (c i) j -> p c j i", i=4),
                 w_raw[o][:].rearrange("p j (c i) -> p c j i", i=4),
@@ -147,9 +140,21 @@ def tile_picked_ysplat_none_p_kernel(
             )
 
         nc.vector.tensor_copy(x_codes[0][:], words[0][:].bitcast(U32).indirect(offs_t[:]))
-        quantise_w(0)
         nc.vector.tensor_copy(x_planes[:], scales[:].indirect(offs_t[:]))
+        quantise_w(0)
         quantise_w(1)
+        last_col = held.tile([P, V_BLOCKS], F32, name="last_col", tag="raw1")
+        look_up_op(D - 1, last_col[:])
+        nc.gpsimd.tensor_tensor(pair[:, :, 3, 0], last_col[:], fall_col[:, :, 3], MULT)
+        nc.gpsimd.tensor_tensor(ct[:, :, 3, 0], pair[:, :, 3, 0], ct[:, :, 2, 1], MULT)
+
+        a0_bank = bank(5)
+        for b in range(V_BLOCKS):
+            nc.tensor.transpose(a0_bank[:, b * P : (b + 1) * P], pair[:, b, 0, 0:1].to_broadcast([P, P]), ident[:])
+        a0_rows = held.tile([P, V], F32, name="a0_rows", tag="raw1")
+        nc.scalar.copy(a0_rows[:], a0_bank[:, 0:V])
+
+        x_codes.append(held.tile([P, S], U32, name="x_codes1", tag="stage1", align_bytes=64))
         h = [held.tile([P, S], F32, name="h%d" % m) for m in range(M_TILES)]
         halves = [slice(0, HALF), slice(HALF, S)]
         h0_banks = [bank(6), bank(7)]
@@ -183,9 +188,12 @@ def tile_picked_ysplat_none_p_kernel(
                         total[m][:, cols], weighted[:, cols], ident[:], is_transpose=True,
                         start=(d == 1 and b == 0), stop=(d == D - 1 and b == V_BLOCKS - 1),
                     )
+        front = []
         for m in range(M_TILES):
             picked = ring.tile([P, V], F32, name="picked")
             nc.vector.tensor_tensor(picked[:], h[m][:].indirect(pos_t[0][:]), a0_rows[:], MULT)
+            front.append(picked)
+        for m in range(M_TILES):
             result = ring.tile([P, V], F32, name="result")
-            nc.vector.tensor_tensor(result[:], total[m][:, 0:V], picked[:], ADD)
+            nc.vector.tensor_tensor(result[:], total[m][:, 0:V], front[m][:], ADD)
             nc.sync.dma_start(out[m * P : (m + 1) * P, :], result[:])

@@ -44,7 +44,7 @@ def tile_picked_ysplat_none_p_kernel(
         fall_t = held.tile([P, V], F32, name="fall_t")
         words = [held.tile([P, T], I32, name="words%d" % o) for o in range(PASSES)]
         scales = held.tile([P, T], U8, name="scales")
-        w_raw = [held.tile([P, PACK, N], F32, name="w_raw%d" % o, tag="raw%d" % o) for o in range(PASSES)]
+        w_raw = [held.tile([P, PACK, N], F32, name="w_raw%d" % o, tag="raw%d" % o, align_bytes=64) for o in range(PASSES)]
         ident = held.tile([P, P], F32, name="ident")
 
         nc.gpsimd.memset(scales[:].bitcast(I32), 0)
@@ -92,31 +92,13 @@ def tile_picked_ysplat_none_p_kernel(
             COPY,
         )
 
-        op_col = held.tile([P, V_BLOCKS, D - 1], F32, name="op_col")
-
-        def look_up_op(d, column):
-            picked = held.tile([P, V], F32, name="op_picked%d" % d)
-            nc.vector.tensor_copy(picked[:], op_t[:].indirect(pos_t[d][:]))
-            turned = bank(1 + d)
-            turn(turned, picked)
-            nc.scalar.copy(column, turned[:, 0:V:P])
-
-        pair = held.tile([P, V_BLOCKS, D, 2], F32, name="pair")
-        ct = held.tile([P, V_BLOCKS, D, 2], F32, name="ct")
-        for d in range(D - 1):
-            look_up_op(d, op_col[:, :, d])
-        nc.gpsimd.tensor_tensor(pair[:, :, 0 : D - 1, 0], op_col[:], fall_col[:, :, 0 : D - 1], MULT)
-        nc.gpsimd.tensor_scalar(pair[:, :, 0 : D - 1, 1], pair[:, :, 0 : D - 1, 0], -1.0, 1.0, MULT, ADD)
-        nc.gpsimd.tensor_tensor(ct[:, :, 1, :], pair[:, :, 1, :], pair[:, :, 0, 1:2].to_broadcast([P, V_BLOCKS, 2]), MULT)
-        nc.gpsimd.tensor_tensor(ct[:, :, 2, :], pair[:, :, 2, :], ct[:, :, 1, 1:2].to_broadcast([P, V_BLOCKS, 2]), MULT)
-
         x_codes = [held.tile([P, S], U32, name="x_codes0", align_bytes=64)]
         x_planes = held.tile([P, S], U8, name="x_planes", align_bytes=64)
         w_codes = [held.tile([P, N], U32, name="w_codes%d" % o, align_bytes=64) for o in range(PASSES)]
         w_planes = [held.tile([P, N], U8, name="w_planes%d" % o, align_bytes=64) for o in range(PASSES)]
 
-        def quantise_w(o):
-            grouped = held.tile([P, N, PACK], BF16, name="grouped%d" % o, tag="stage%d" % o, align_bytes=64)
+        def quantise_w(o, tag):
+            grouped = held.tile([P, N, PACK], BF16, name="grouped%d" % o, tag=tag, align_bytes=64)
             nc.scalar.activation(
                 grouped[:].rearrange("p (c i) j -> p c j i", i=4),
                 w_raw[o][:].rearrange("p j (c i) -> p c j i", i=4),
@@ -139,22 +121,44 @@ def tile_picked_ysplat_none_p_kernel(
                 stop=(o == PASSES - 1),
             )
 
+        def look_up_op(d):
+            picked = held.tile([P, V], F32, name="op_picked%d" % d)
+            nc.vector.tensor_copy(picked[:], op_t[:].indirect(pos_t[d][:]))
+            turned = bank(1 + d)
+            turn(turned, picked)
+            return turned
+
+        op_col = held.tile([P, V_BLOCKS, D - 1], F32, name="op_col", tag="columns", align_bytes=64)
+        pair = held.tile([P, V_BLOCKS, D - 1, 2], F32, name="pair")
+        ct = held.tile([P, V_BLOCKS, D - 1, 2], F32, name="ct")
+        seen = held.tile([P, V_BLOCKS], F32, name="seen")
+        for d in range(D - 1):
+            nc.scalar.copy(op_col[:, :, d], look_up_op(d)[:, 0:V:P])
+        nc.gpsimd.tensor_tensor(pair[:, :, :, 0], op_col[:], fall_col[:, :, 0 : D - 1], MULT)
+        nc.gpsimd.tensor_scalar(pair[:, :, :, 1], pair[:, :, :, 0], -1.0, 1.0, MULT, ADD)
+        nc.gpsimd.tensor_tensor(ct[:, :, 1, :], pair[:, :, 1, :], pair[:, :, 0, 1:2].to_broadcast([P, V_BLOCKS, 2]), MULT)
+        nc.gpsimd.tensor_tensor(ct[:, :, 2, :], pair[:, :, 2, :], ct[:, :, 1, 1:2].to_broadcast([P, V_BLOCKS, 2]), MULT)
+        nc.gpsimd.tensor_tensor(seen[:], fall_col[:, :, D - 1], ct[:, :, 2, 1], MULT)
+
         nc.vector.tensor_copy(x_codes[0][:], words[0][:].bitcast(U32).indirect(offs_t[:]))
         nc.vector.tensor_copy(x_planes[:], scales[:].indirect(offs_t[:]))
-        quantise_w(0)
-        quantise_w(1)
-        last_col = held.tile([P, V_BLOCKS], F32, name="last_col", tag="raw1")
-        look_up_op(D - 1, last_col[:])
-        nc.gpsimd.tensor_tensor(pair[:, :, 3, 0], last_col[:], fall_col[:, :, 3], MULT)
-        nc.gpsimd.tensor_tensor(ct[:, :, 3, 0], pair[:, :, 3, 0], ct[:, :, 2, 1], MULT)
+        quantise_w(0, "columns")
+        quantise_w(1, "raw0")
+        last_turned = look_up_op(D - 1)
+        x_codes.append(held.tile([P, S], U32, name="x_codes1", tag="raw0", align_bytes=64))
 
-        a0_bank = bank(5)
+        last = held.tile([P, V_BLOCKS], F32, name="last")
         for b in range(V_BLOCKS):
-            nc.tensor.transpose(a0_bank[:, b * P : (b + 1) * P], pair[:, b, 0, 0:1].to_broadcast([P, P]), ident[:])
-        a0_rows = held.tile([P, V], F32, name="a0_rows", tag="raw1")
-        nc.scalar.copy(a0_rows[:], a0_bank[:, 0:V])
+            nc.scalar.activation(last[:, b : b + 1], last_turned[:, b * P : b * P + 1], COPY, scale=seen[:, b : b + 1])
+        weight_columns = [pair[:, :, 0, 0], ct[:, :, 1, 0], ct[:, :, 2, 0], last[:]]
+        weight_rows = held.tile([P, D * V], F32, name="weight_rows", tag="raw1", align_bytes=64)
+        for d in range(D):
+            spread_bank = bank(1 + d)
+            for b in range(V_BLOCKS):
+                column = weight_columns[d][:, b : b + 1]
+                nc.tensor.transpose(spread_bank[:, b * P : (b + 1) * P], column.to_broadcast([P, P]), ident[:])
+            nc.scalar.copy(weight_rows[:, d * V : (d + 1) * V], spread_bank[:, 0:V])
 
-        x_codes.append(held.tile([P, S], U32, name="x_codes1", tag="stage1", align_bytes=64))
         h = [held.tile([P, S], F32, name="h%d" % m) for m in range(M_TILES)]
         halves = [slice(0, HALF), slice(HALF, S)]
         h0_banks = [bank(6), bank(7)]
@@ -171,29 +175,28 @@ def tile_picked_ysplat_none_p_kernel(
         product_pass(h1_bank[:], 1, 1, slice(0, S))
         nc.scalar.copy(h[1][:], h1_bank[:])
 
-        total = [bank(5 + m) for m in range(M_TILES)]
+        total = []
         for m in range(M_TILES):
-            for d in range(1, D):
+            summed_bank = bank(5 + m)
+            for d in range(D - 1):
                 picked = ring.tile([P, V], F32, name="picked")
-                nc.vector.tensor_copy(picked[:], h[m][:].indirect(pos_t[d][:]))
-                turned = bank(d)
-                turn(turned, picked)
-                weighted = ring.tile([P, V], F32, name="weighted")
-                for b in range(V_BLOCKS):
-                    cols = slice(b * P, (b + 1) * P)
-                    nc.scalar.activation(weighted[:, cols], turned[:, cols], COPY, scale=ct[:, b, d, 0:1])
+                nc.vector.tensor_tensor(picked[:], h[m][:].indirect(pos_t[d][:]), weight_rows[:, d * V : (d + 1) * V], MULT)
                 for b in range(V_BLOCKS):
                     cols = slice(b * P, (b + 1) * P)
                     nc.tensor.matmul(
-                        total[m][:, cols], weighted[:, cols], ident[:], is_transpose=True,
-                        start=(d == 1 and b == 0), stop=(d == D - 1 and b == V_BLOCKS - 1),
+                        summed_bank[:, cols], picked[:, cols], ident[:], is_transpose=True,
+                        start=(d == 0 and b == 0), stop=(d == D - 2 and b == V_BLOCKS - 1),
                     )
-        front = []
+            summed = ring.tile([P, V], F32, name="summed")
+            nc.scalar.copy(summed[:], summed_bank[:, 0:V])
+            total.append(bank(1 + m))
+            turn(total[m], summed)
+        back = []
         for m in range(M_TILES):
             picked = ring.tile([P, V], F32, name="picked")
-            nc.vector.tensor_tensor(picked[:], h[m][:].indirect(pos_t[0][:]), a0_rows[:], MULT)
-            front.append(picked)
+            nc.vector.tensor_tensor(picked[:], h[m][:].indirect(pos_t[D - 1][:]), weight_rows[:, (D - 1) * V : D * V], MULT)
+            back.append(picked)
         for m in range(M_TILES):
             result = ring.tile([P, V], F32, name="result")
-            nc.vector.tensor_tensor(result[:], total[m][:, 0:V], front[m][:], ADD)
+            nc.vector.tensor_tensor(result[:], total[m][:, 0:V], back[m][:], ADD)
             nc.sync.dma_start(out[m * P : (m + 1) * P, :], result[:])

@@ -61,7 +61,14 @@ def tile_picked_ysplat_none_p_kernel(
             rows = w1[o * 512 : (o + 1) * 512, :]
             nc.sync.dma_start(w_raw[o][:], rows.rearrange("(p j) n -> p j n", j=PACK))
 
+        def load_scales(q, passes):
+            nc.sync.dma_start(
+                scales[32 * q + 4 * passes.start : 32 * q + 4 * passes.stop, :].bitcast(I32),
+                x_scales[passes, 4 * q : 4 * q + 4, :].bitcast(I32),
+            )
+
         fall_rows = fall.rearrange("d p v -> (d p) v")
+        load_w(0)
         nc.sync.dma_start(op_t[0:ROWS, :], op[0:ROWS, :])
         nc.sync.dma_start(pos_t[0][:], pos1)
         nc.sync.dma_start(fall_t[64 : 64 + ROWS, :], fall_rows[0 : D * P : D * P // ROWS, :])
@@ -69,14 +76,12 @@ def tile_picked_ysplat_none_p_kernel(
         nc.sync.dma_start(pos_t[2][:], pos3)
         nc.sync.dma_start(offs_t[:], offs)
         load_words(0)
-        load_w(0)
-        nc.sync.dma_start(pos_t[3][:], pos4)
-        for q in range(4):
-            nc.sync.dma_start(
-                scales[32 * q : 32 * q + 4 * PASSES, :].bitcast(I32),
-                x_scales[:, 4 * q : 4 * q + 4, :].bitcast(I32),
-            )
         load_w(1)
+        nc.sync.dma_start(pos_t[3][:], pos4)
+        for q in range(3):
+            load_scales(q, slice(0, PASSES))
+        for o in range(PASSES):
+            load_scales(3, slice(o, o + 1))
         load_words(1)
 
         def turn(dst_bank, src):
@@ -140,12 +145,12 @@ def tile_picked_ysplat_none_p_kernel(
         nc.gpsimd.tensor_tensor(ct[:, :, 2, :], pair[:, :, 2, :], ct[:, :, 1, 1:2].to_broadcast([P, V_BLOCKS, 2]), MULT)
         nc.gpsimd.tensor_tensor(seen[:], fall_col[:, :, D - 1], ct[:, :, 2, 1], MULT)
 
+        quantise_w(0, "grouped0")
         nc.vector.tensor_copy(x_codes[0][:], words[0][:].bitcast(U32).indirect(offs_t[:]))
-        nc.vector.tensor_copy(x_planes[:], scales[:].indirect(offs_t[:]))
-        quantise_w(0, "columns")
-        quantise_w(1, "raw0")
         last_turned = look_up_op(D - 1)
-        x_codes.append(held.tile([P, S], U32, name="x_codes1", tag="raw0", align_bytes=64))
+        nc.vector.tensor_copy(x_planes[:], scales[:].indirect(offs_t[:]))
+        quantise_w(1, "columns")
+        x_codes.append(held.tile([P, S], U32, name="x_codes1", tag="columns", align_bytes=64))
 
         last = held.tile([P, V_BLOCKS], F32, name="last")
         for b in range(V_BLOCKS):

@@ -40,168 +40,175 @@ def tile_picked_ysplat_none_p_kernel(
 
         offs_t = held.tile([P, S // 16], U16, name="offs_t")
         pos_t = [held.tile([P, V // 16], U16, name="pos_t%d" % d) for d in range(D)]
+        pos = [pos1, pos2, pos3, pos4]
         op_t = held.tile([P, S], F32, name="op_t")
         fall_t = held.tile([P, V], F32, name="fall_t")
-        words = [held.tile([P, T], I32, name="words%d" % o) for o in range(PASSES)]
-        scales = held.tile([P, T], U8, name="scales")
-        w_raw = [held.tile([P, PACK, N], F32, name="w_raw%d" % o, tag="raw%d" % o, align_bytes=64) for o in range(PASSES)]
+        words = [held.tile([P, T], I32, name="words%d" % o, tag="words%d" % o, align_bytes=64) for o in range(PASSES)]
+        scales = held.tile([P, T], U8, name="scales", tag="scales", align_bytes=64)
+        w_raw = [held.tile([P, PACK, N], F32, name="w_raw0", align_bytes=64)]
+        w_last = [held.tile([P, PACK, P], F32, name="w_last%d" % m, tag="w_last%d" % m, align_bytes=64) for m in range(M_TILES)]
         ident = held.tile([P, P], F32, name="ident")
 
         nc.gpsimd.memset(scales[:].bitcast(I32), 0)
         make_identity(nc, ident[:])
         nc.vector.memset(op_t[32:64, :], 0.0)
         nc.vector.memset(op_t[64:128, :], 0.0)
-        nc.vector.memset(fall_t[0:64, :], 0.0)
-        nc.vector.memset(fall_t[96:128, :], 0.0)
+        nc.vector.memset(fall_t[32:64, :], 0.0)
+        nc.vector.memset(fall_t[64:128, :], 0.0)
 
-        def load_words(o):
-            nc.sync.dma_start(words[o][:], x_words[o].rearrange("p c r -> p (c r)").bitcast(I32))
+        def load_words(o, q=nc.sync):
+            q.dma_start(words[o][:], x_words[o].rearrange("p c r -> p (c r)").bitcast(I32))
 
-        def load_w(o):
+        def load_w(o, q=nc.sync):
             rows = w1[o * 512 : (o + 1) * 512, :]
-            nc.sync.dma_start(w_raw[o][:], rows.rearrange("(p j) n -> p j n", j=PACK))
+            q.dma_start(w_raw[o][:], rows.rearrange("(p j) n -> p j n", j=PACK))
 
-        def load_scales(q, passes):
-            nc.sync.dma_start(
+        def load_w_tile(m):
+            rows = w1[512:1024, m * P : (m + 1) * P]
+            nc.sync.dma_start(w_last[m][:], rows.rearrange("(p j) n -> p j n", j=PACK))
+
+        def load_scales(q, passes, queue=nc.sync):
+            queue.dma_start(
                 scales[32 * q + 4 * passes.start : 32 * q + 4 * passes.stop, :].bitcast(I32),
                 x_scales[passes, 4 * q : 4 * q + 4, :].bitcast(I32),
             )
 
-        fall_rows = fall.rearrange("d p v -> (d p) v")
+        def load_op(q=nc.sync):
+            q.dma_start(op_t[0:ROWS, :], op[0:ROWS, :])
+
+        def load_fall(q=nc.sync):
+            fall_rows = fall.rearrange("d p v -> (d p) v")
+            q.dma_start(fall_t[0:ROWS, :], fall_rows[0 : D * P : D * P // ROWS, :])
+
+        def load_pos(d):
+            nc.sync.dma_start(pos_t[d][:], pos[d])
+
+        def load_offs():
+            nc.sync.dma_start(offs_t[:], offs)
+
+        both = slice(0, PASSES)
         load_w(0)
-        nc.sync.dma_start(op_t[0:ROWS, :], op[0:ROWS, :])
-        nc.sync.dma_start(pos_t[0][:], pos1)
-        nc.sync.dma_start(fall_t[64 : 64 + ROWS, :], fall_rows[0 : D * P : D * P // ROWS, :])
-        nc.sync.dma_start(pos_t[1][:], pos2)
-        nc.sync.dma_start(pos_t[2][:], pos3)
-        nc.sync.dma_start(offs_t[:], offs)
+        load_op()
+        load_fall()
+        for d in range(D):
+            load_pos(d)
         load_words(0)
-        load_w(1)
-        nc.sync.dma_start(pos_t[3][:], pos4)
-        for q in range(3):
-            load_scales(q, slice(0, PASSES))
-        for o in range(PASSES):
-            load_scales(3, slice(o, o + 1))
+        load_offs()
+        for q in range(4):
+            load_scales(q, both)
+        load_w_tile(0)
         load_words(1)
+        load_w_tile(1)
 
-        def turn(dst_bank, src):
+        def turn(dst, src):
             for b in range(V_BLOCKS):
-                nc.tensor.transpose(dst_bank[:, b * P : (b + 1) * P], src[:, b * P : (b + 1) * P], ident[:])
+                nc.tensor.transpose(dst[:, b * P : (b + 1) * P], src[:, b * P : (b + 1) * P], ident[:])
 
-        fall_bank = bank(0)
-        turn(fall_bank, fall_t)
-        fall_col = held.tile([P, V_BLOCKS, D], F32, name="fall_col")
-        nc.scalar.activation(
-            fall_col[:],
-            fall_bank[:, 0:V].rearrange("p (b r) -> p b r", b=V_BLOCKS)[:, :, 64 : 64 + ROWS : ROWS // D],
-            COPY,
-        )
+        turned = [bank(0), bank(1)]
+        for d in range(D):
+            a_rows = held.tile([P, V], F32, name="a_rows%d" % d, tag="a_rows%d" % d, align_bytes=64)
+            nc.vector.tensor_tensor(a_rows[:], op_t[:].indirect(pos_t[d][:]), fall_t[:], MULT)
+            turn(turned[d // 2][:, (d % 2) * V : (d % 2 + 1) * V], a_rows)
 
-        x_codes = [held.tile([P, S], U32, name="x_codes0", align_bytes=64)]
-        x_planes = held.tile([P, S], U8, name="x_planes", align_bytes=64)
-        w_codes = [held.tile([P, N], U32, name="w_codes%d" % o, align_bytes=64) for o in range(PASSES)]
-        w_planes = [held.tile([P, N], U8, name="w_planes%d" % o, align_bytes=64) for o in range(PASSES)]
+        x_codes = [held.tile([P, S], U32, name="x_codes%d" % o, align_bytes=64) for o in range(PASSES)]
+        w_codes = {}
+        w_planes = {}
 
-        def quantise_w(o, tag):
-            grouped = held.tile([P, N, PACK], BF16, name="grouped%d" % o, tag=tag, align_bytes=64)
-            nc.scalar.activation(
-                grouped[:].rearrange("p (c i) j -> p c j i", i=4),
-                w_raw[o][:].rearrange("p j (c i) -> p c j i", i=4),
-                COPY,
-            )
-            nc.vector.quantize_mx(
-                out=w_codes[o][:].bitcast(FP8X4),
-                scales=w_planes[o][:],
-                in_=grouped[:].rearrange("p n j -> p (n j)"),
-            )
+        def group_w(raw, name, tag, on_vector=False):
+            grouped = held.tile([P, raw.shape[2], PACK], BF16, name=name, tag=tag, align_bytes=64)
+            dst = grouped[:].rearrange("p (c i) j -> p c j i", i=4)
+            src = raw[:].rearrange("p j (c i) -> p c j i", i=4)
+            if on_vector:
+                nc.vector.tensor_copy(dst, src)
+            else:
+                nc.scalar.activation(dst, src, COPY)
+            return grouped
+
+        def quantise_w(grouped, o, tiles, tag):
+            width = len(tiles) * P
+            codes = held.tile([P, width], U32, name="w_codes%d_%d" % (o, tiles[0]), align_bytes=64)
+            planes = held.tile([P, width], U8, name="w_planes%d_%d" % (o, tiles[0]), tag=tag, align_bytes=64)
+            nc.vector.quantize_mx(out=codes[:].bitcast(FP8X4), scales=planes[:], in_=grouped[:].rearrange("p n j -> p (n j)"))
+            for i, m in enumerate(tiles):
+                w_codes[o, m] = codes[:, i * P : (i + 1) * P]
+                w_planes[o, m] = planes[:, i * P : (i + 1) * P]
 
         def product_pass(acc, m, o, cols):
             nc.tensor.matmul_mx(
                 out=acc,
-                lhsT=w_codes[o][:, m * P : (m + 1) * P].bitcast(FP8X4),
-                lhsT_scale=w_planes[o][:, m * P : (m + 1) * P],
+                lhsT=w_codes[o, m].bitcast(FP8X4),
+                lhsT_scale=w_planes[o, m],
                 rhs=x_codes[o][:, cols].bitcast(FP8X4),
                 rhs_scale=x_planes[4 * o : P, cols],
                 start=(o == 0),
                 stop=(o == PASSES - 1),
             )
 
-        def look_up_op(d):
-            picked = held.tile([P, V], F32, name="op_picked%d" % d)
-            nc.vector.tensor_copy(picked[:], op_t[:].indirect(pos_t[d][:]))
-            turned = bank(1 + d)
-            turn(turned, picked)
-            return turned
+        quantise_w(group_w(w_raw[0], "grouped0", "grouped0"), 0, [0, 1], "w_planes0")
 
-        op_col = held.tile([P, V_BLOCKS, D - 1], F32, name="op_col", tag="columns", align_bytes=64)
-        pair = held.tile([P, V_BLOCKS, D - 1, 2], F32, name="pair")
-        ct = held.tile([P, V_BLOCKS, D - 1, 2], F32, name="ct")
-        seen = held.tile([P, V_BLOCKS], F32, name="seen")
-        for d in range(D - 1):
-            nc.scalar.copy(op_col[:, :, d], look_up_op(d)[:, 0:V:P])
-        nc.gpsimd.tensor_tensor(pair[:, :, :, 0], op_col[:], fall_col[:, :, 0 : D - 1], MULT)
-        nc.gpsimd.tensor_scalar(pair[:, :, :, 1], pair[:, :, :, 0], -1.0, 1.0, MULT, ADD)
-        nc.gpsimd.tensor_tensor(ct[:, :, 1, :], pair[:, :, 1, :], pair[:, :, 0, 1:2].to_broadcast([P, V_BLOCKS, 2]), MULT)
-        nc.gpsimd.tensor_tensor(ct[:, :, 2, :], pair[:, :, 2, :], ct[:, :, 1, 1:2].to_broadcast([P, V_BLOCKS, 2]), MULT)
-        nc.gpsimd.tensor_tensor(seen[:], fall_col[:, :, D - 1], ct[:, :, 2, 1], MULT)
+        pair = held.tile([P, D, V_BLOCKS, 2], F32, name="pair")
+        ct = held.tile([P, D, V_BLOCKS, 2], F32, name="ct")
+        step = P + 4
+        for i in range(2):
+            nc.scalar.copy(pair[:, 2 * i : 2 * i + 2, :, 0].rearrange("p d b -> p (d b)"), turned[i][:, 16 * i : 512 : step])
+        nc.gpsimd.tensor_scalar(pair[:, 0 : D - 1, :, 1], pair[:, 0 : D - 1, :, 0], -1.0, 1.0, MULT, ADD)
+        nc.gpsimd.tensor_tensor(ct[:, 1, :, :], pair[:, 1, :, :], pair[:, 0, :, 1:2].to_broadcast([P, V_BLOCKS, 2]), MULT)
+        nc.gpsimd.tensor_tensor(ct[:, 2, :, :], pair[:, 2, :, :], ct[:, 1, :, 1:2].to_broadcast([P, V_BLOCKS, 2]), MULT)
+        nc.gpsimd.tensor_tensor(ct[:, 3, :, 0], pair[:, 3, :, 0], ct[:, 2, :, 1], MULT)
+        grouped1 = group_w(w_last[0], "grouped1", "a_rows3")
+        weight_rows = held.tile([P, D * V], F32, name="weight_rows", tag="w_last0", align_bytes=64)
+        for i in range(2):
+            spread_bank = bank(2 + i)
+            for c in range(4):
+                source = pair if (i == 0 and c < 2) else ct
+                column = source[:, 2 * i + c // 2, c % 2, 0:1]
+                nc.tensor.transpose(spread_bank[:, c * P : (c + 1) * P], column.to_broadcast([P, P]), ident[:])
+            nc.scalar.copy(weight_rows[:, i * 512 : (i + 1) * 512], spread_bank[:])
 
-        quantise_w(0, "grouped0")
         nc.vector.tensor_copy(x_codes[0][:], words[0][:].bitcast(U32).indirect(offs_t[:]))
-        last_turned = look_up_op(D - 1)
+        x_planes = held.tile([P, S], U8, name="x_planes", tag="words0", align_bytes=64)
         nc.vector.tensor_copy(x_planes[:], scales[:].indirect(offs_t[:]))
-        quantise_w(1, "columns")
-        x_codes.append(held.tile([P, S], U32, name="x_codes1", tag="columns", align_bytes=64))
-
-        last = held.tile([P, V_BLOCKS], F32, name="last")
-        for b in range(V_BLOCKS):
-            nc.scalar.activation(last[:, b : b + 1], last_turned[:, b * P : b * P + 1], COPY, scale=seen[:, b : b + 1])
-        weight_columns = [pair[:, :, 0, 0], ct[:, :, 1, 0], ct[:, :, 2, 0], last[:]]
-        weight_rows = held.tile([P, D * V], F32, name="weight_rows", tag="raw1", align_bytes=64)
-        for d in range(D):
-            spread_bank = bank(1 + d)
-            for b in range(V_BLOCKS):
-                column = weight_columns[d][:, b : b + 1]
-                nc.tensor.transpose(spread_bank[:, b * P : (b + 1) * P], column.to_broadcast([P, P]), ident[:])
-            nc.scalar.copy(weight_rows[:, d * V : (d + 1) * V], spread_bank[:, 0:V])
+        quantise_w(grouped1, 1, [0], "scales")
 
         h = [held.tile([P, S], F32, name="h%d" % m) for m in range(M_TILES)]
-        halves = [slice(0, HALF), slice(HALF, S)]
-        h0_banks = [bank(6), bank(7)]
-        h1_bank = bank(0)
-        for i in range(2):
-            product_pass(h0_banks[i][:, 0:HALF], 0, 0, halves[i])
+        pieces = [slice(0, HALF), slice(HALF, S)]
+        h0_banks = [bank(4 + i)[:, 0 : piece.stop - piece.start] for i, piece in enumerate(pieces)]
+        h1_bank = bank(6)
+        for i, piece in enumerate(pieces):
+            product_pass(h0_banks[i], 0, 0, piece)
         product_pass(h1_bank[:], 1, 0, slice(0, S))
-        for i in range(2):
+        for i, piece in enumerate(pieces):
             nc.vector.tensor_copy(
-                x_codes[1][:, halves[i]], words[1][:].bitcast(U32).indirect(offs_t[:, i * HALF // 16 : (i + 1) * HALF // 16])
+                x_codes[1][:, piece], words[1][:].bitcast(U32).indirect(offs_t[:, piece.start // 16 : piece.stop // 16])
             )
-            product_pass(h0_banks[i][:, 0:HALF], 0, 1, halves[i])
-            nc.scalar.copy(h[0][:, halves[i]], h0_banks[i][:, 0:HALF])
+            product_pass(h0_banks[i], 0, 1, piece)
+            nc.scalar.copy(h[0][:, piece], h0_banks[i])
+        quantise_w(group_w(w_last[1], "grouped2", "words1", on_vector=True), 1, [1], "w_planes2")
         product_pass(h1_bank[:], 1, 1, slice(0, S))
         nc.scalar.copy(h[1][:], h1_bank[:])
 
         total = []
         for m in range(M_TILES):
-            summed_bank = bank(5 + m)
+            sum_banks = [bank(4 * m + b) for b in range(V_BLOCKS)]
             for d in range(D - 1):
                 picked = ring.tile([P, V], F32, name="picked")
                 nc.vector.tensor_tensor(picked[:], h[m][:].indirect(pos_t[d][:]), weight_rows[:, d * V : (d + 1) * V], MULT)
                 for b in range(V_BLOCKS):
-                    cols = slice(b * P, (b + 1) * P)
                     nc.tensor.matmul(
-                        summed_bank[:, cols], picked[:, cols], ident[:], is_transpose=True,
-                        start=(d == 0 and b == 0), stop=(d == D - 2 and b == V_BLOCKS - 1),
+                        sum_banks[b][:, 0:P], picked[:, b * P : (b + 1) * P], ident[:], is_transpose=True,
+                        start=(d == 0), stop=(d == D - 2),
                     )
-            summed = ring.tile([P, V], F32, name="summed")
-            nc.scalar.copy(summed[:], summed_bank[:, 0:V])
-            total.append(bank(1 + m))
-            turn(total[m], summed)
+            total.append(bank(2 + m))
+            for b in range(V_BLOCKS):
+                summed = held.tile([P, P], F32, name="summed%d_%d" % (m, b))
+                nc.scalar.copy(summed[:], sum_banks[b][:, 0:P])
+                nc.tensor.transpose(total[m][:, b * P : (b + 1) * P], summed[:], ident[:])
         back = []
         for m in range(M_TILES):
             picked = ring.tile([P, V], F32, name="picked")
             nc.vector.tensor_tensor(picked[:], h[m][:].indirect(pos_t[D - 1][:]), weight_rows[:, (D - 1) * V : D * V], MULT)
             back.append(picked)
-        for m in range(M_TILES):
-            result = ring.tile([P, V], F32, name="result")
-            nc.vector.tensor_tensor(result[:], total[m][:, 0:V], back[m][:], ADD)
-            nc.sync.dma_start(out[m * P : (m + 1) * P, :], result[:])
+        for m, cols in [(0, slice(0, V)), (1, slice(0, P)), (1, slice(P, V))]:
+            result = ring.tile([P, cols.stop - cols.start], F32, name="result")
+            nc.vector.tensor_tensor(result[:], total[m][:, cols], back[m][:, cols], ADD)
+            nc.sync.dma_start(out[m * P : (m + 1) * P, cols], result[:])

@@ -45,11 +45,11 @@ def tile_picked_ysplat_none_p_kernel(
         fall_t = held.tile([P, V], F32, name="fall_t")
         words = [held.tile([P, T], I32, name="words%d" % o, tag="words%d" % o, align_bytes=64) for o in range(PASSES)]
         scales = held.tile([P, T], U8, name="scales", tag="scales", align_bytes=64)
-        w_raw = [held.tile([P, PACK, N], F32, name="w_raw0", align_bytes=64)]
-        w_last = [held.tile([P, PACK, P], F32, name="w_last%d" % m, tag="w_last%d" % m, align_bytes=64) for m in range(M_TILES)]
+        w_raw = [held.tile([P, PACK, N], F32, name="w_raw%d" % o, tag="w_raw%d" % o, align_bytes=64) for o in range(PASSES)]
         ident = held.tile([P, P], F32, name="ident")
 
-        nc.gpsimd.memset(scales[:].bitcast(I32), 0)
+        nc.gpsimd.memset(scales[32:64, :].bitcast(I32), 0)
+        nc.gpsimd.memset(scales[64:128, :].bitcast(I32), 0)
         make_identity(nc, ident[:])
         nc.vector.memset(op_t[32:64, :], 0.0)
         nc.vector.memset(op_t[64:128, :], 0.0)
@@ -62,16 +62,6 @@ def tile_picked_ysplat_none_p_kernel(
         def load_w(o, q=nc.sync):
             rows = w1[o * 512 : (o + 1) * 512, :]
             q.dma_start(w_raw[o][:], rows.rearrange("(p j) n -> p j n", j=PACK))
-
-        def load_w_tile(m):
-            rows = w1[512:1024, m * P : (m + 1) * P]
-            nc.sync.dma_start(w_last[m][:], rows.rearrange("(p j) n -> p j n", j=PACK))
-
-        def load_scales(q, passes, queue=nc.sync):
-            queue.dma_start(
-                scales[32 * q + 4 * passes.start : 32 * q + 4 * passes.stop, :].bitcast(I32),
-                x_scales[passes, 4 * q : 4 * q + 4, :].bitcast(I32),
-            )
 
         def load_op(q=nc.sync):
             q.dma_start(op_t[0:ROWS, :], op[0:ROWS, :])
@@ -86,31 +76,37 @@ def tile_picked_ysplat_none_p_kernel(
         def load_offs():
             nc.sync.dma_start(offs_t[:], offs)
 
-        both = slice(0, PASSES)
         load_w(0)
         load_op()
         load_fall()
-        for d in range(D):
-            load_pos(d)
-        load_words(0)
+        load_pos(0)
+        load_pos(1)
+        nc.sync.dma_start(scales[0:32, :].bitcast(I32), x_scales.rearrange("o q c -> (o q) c").bitcast(I32))
         load_offs()
-        for q in range(4):
-            load_scales(q, both)
-        load_w_tile(0)
+        load_words(0)
+        load_pos(2)
+        load_pos(3)
+        load_w(1)
         load_words(1)
-        load_w_tile(1)
 
         def turn(dst, src):
             for b in range(V_BLOCKS):
                 nc.tensor.transpose(dst[:, b * P : (b + 1) * P], src[:, b * P : (b + 1) * P], ident[:])
 
         turned = [bank(0), bank(1)]
-        for d in range(D):
-            a_rows = held.tile([P, V], F32, name="a_rows%d" % d, tag="a_rows%d" % d, align_bytes=64)
-            nc.vector.tensor_tensor(a_rows[:], op_t[:].indirect(pos_t[d][:]), fall_t[:], MULT)
-            turn(turned[d // 2][:, (d % 2) * V : (d % 2 + 1) * V], a_rows)
 
-        x_codes = [held.tile([P, S], U32, name="x_codes%d" % o, align_bytes=64) for o in range(PASSES)]
+        def look_up_op(d, tag, dst):
+            a_rows = held.tile([P, V], F32, name="a_rows%d" % d, tag=tag, align_bytes=64)
+            nc.vector.tensor_tensor(a_rows[:], op_t[:].indirect(pos_t[d][:]), fall_t[:], MULT)
+            turn(dst, a_rows)
+
+
+        for d in range(2):
+            look_up_op(d, "a_rows%d" % d, turned[0][:, d * V : (d + 1) * V])
+        x_rows = held.tile([P, S], U8, name="x_rows", align_bytes=64)
+        nc.vector.tensor_copy(x_rows[:], scales[:].indirect(offs_t[:]))
+
+        x_codes = [held.tile([P, S], U32, name="x_codes0", align_bytes=64)]
         w_codes = {}
         w_planes = {}
 
@@ -144,31 +140,45 @@ def tile_picked_ysplat_none_p_kernel(
                 stop=(o == PASSES - 1),
             )
 
-        quantise_w(group_w(w_raw[0], "grouped0", "grouped0"), 0, [0, 1], "w_planes0")
+        grouped0 = group_w(w_raw[0], "grouped0", "grouped0")
+        x_planes = held.tile([P, S], U8, name="x_planes", tag="w_raw0", align_bytes=64)
+        nc.vector.tensor_copy(x_planes[:].bitcast(I32), x_rows[:].bitcast(I32))
+        for o in range(PASSES):
+            for q in range(4):
+                if o + q > 0:
+                    nc.scalar.dma_start(
+                        x_planes[32 * q + 4 * o : 32 * q + 4 * o + 4, :].bitcast(I32),
+                        x_rows[16 * o + 4 * q : 16 * o + 4 * q + 4, :].bitcast(I32),
+                    )
+        quantise_w(grouped0, 0, [0, 1], "w_planes0")
+        look_up_op(2, "a_rows2", turned[1][:, 0:V])
 
-        pair = held.tile([P, D, V_BLOCKS, 2], F32, name="pair")
-        ct = held.tile([P, D, V_BLOCKS, 2], F32, name="ct")
+        pair = held.tile([P, 2, V_BLOCKS, 2], F32, name="pair")
+        ct = held.tile([P, 2, V_BLOCKS, 2], F32, name="ct")
         step = P + 4
-        for i in range(2):
-            nc.scalar.copy(pair[:, 2 * i : 2 * i + 2, :, 0].rearrange("p d b -> p (d b)"), turned[i][:, 16 * i : 512 : step])
-        nc.gpsimd.tensor_scalar(pair[:, 0 : D - 1, :, 1], pair[:, 0 : D - 1, :, 0], -1.0, 1.0, MULT, ADD)
-        nc.gpsimd.tensor_tensor(ct[:, 1, :, :], pair[:, 1, :, :], pair[:, 0, :, 1:2].to_broadcast([P, V_BLOCKS, 2]), MULT)
-        nc.gpsimd.tensor_tensor(ct[:, 2, :, :], pair[:, 2, :, :], ct[:, 1, :, 1:2].to_broadcast([P, V_BLOCKS, 2]), MULT)
-        nc.gpsimd.tensor_tensor(ct[:, 3, :, 0], pair[:, 3, :, 0], ct[:, 2, :, 1], MULT)
-        grouped1 = group_w(w_last[0], "grouped1", "a_rows3")
-        weight_rows = held.tile([P, D * V], F32, name="weight_rows", tag="w_last0", align_bytes=64)
-        for i in range(2):
-            spread_bank = bank(2 + i)
-            for c in range(4):
-                source = pair if (i == 0 and c < 2) else ct
-                column = source[:, 2 * i + c // 2, c % 2, 0:1]
-                nc.tensor.transpose(spread_bank[:, c * P : (c + 1) * P], column.to_broadcast([P, P]), ident[:])
-            nc.scalar.copy(weight_rows[:, i * 512 : (i + 1) * 512], spread_bank[:])
+        nc.scalar.copy(pair[:, :, :, 0].rearrange("p d b -> p (d b)"), turned[0][:, 0:512:step])
+        nc.gpsimd.tensor_scalar(pair[:, :, :, 1], pair[:, :, :, 0], -1.0, 1.0, MULT, ADD)
+        nc.gpsimd.tensor_tensor(ct[:, 0, :, :], pair[:, 1, :, :], pair[:, 0, :, 1:2].to_broadcast([P, V_BLOCKS, 2]), MULT)
 
         nc.vector.tensor_copy(x_codes[0][:], words[0][:].bitcast(U32).indirect(offs_t[:]))
-        x_planes = held.tile([P, S], U8, name="x_planes", tag="words0", align_bytes=64)
-        nc.vector.tensor_copy(x_planes[:], scales[:].indirect(offs_t[:]))
-        quantise_w(grouped1, 1, [0], "scales")
+        quantise_w(group_w(w_raw[1], "grouped1", "grouped1"), 1, [0, 1], "w_planes1")
+        x_codes.append(held.tile([P, S], U32, name="x_codes1", tag="grouped1", align_bytes=64))
+
+        late = held.tile([P, D * V + 2 * V_BLOCKS], F32, name="late", tag="w_raw1", align_bytes=64)
+        weight_rows = late[:, 0 : D * V]
+        third = late[:, D * V : D * V + 2 * V_BLOCKS].rearrange("p (b i) -> p b i", i=2)
+        nc.scalar.copy(third[:, :, 0], turned[1][:, 16:256:step])
+        nc.gpsimd.tensor_scalar(third[:, :, 1], third[:, :, 0], -1.0, 1.0, MULT, ADD)
+        nc.gpsimd.tensor_tensor(ct[:, 1, :, :], third, ct[:, 0, :, 1:2].to_broadcast([P, V_BLOCKS, 2]), MULT)
+
+        def spread(index, columns, first):
+            spread_bank = bank(index)
+            for c, column in enumerate(columns):
+                nc.tensor.transpose(spread_bank[:, c * P : (c + 1) * P], column.to_broadcast([P, P]), ident[:])
+            nc.scalar.copy(weight_rows[:, first * P : (first + len(columns)) * P], spread_bank[:, 0 : len(columns) * P])
+
+        spread(2, [pair[:, 0, 0, 0:1], pair[:, 0, 1, 0:1], ct[:, 0, 0, 0:1], ct[:, 0, 1, 0:1]], 0)
+        spread(3, [ct[:, 1, 0, 0:1], ct[:, 1, 1, 0:1]], 4)
 
         h = [held.tile([P, S], F32, name="h%d" % m) for m in range(M_TILES)]
         pieces = [slice(0, HALF), slice(HALF, S)]
@@ -183,9 +193,14 @@ def tile_picked_ysplat_none_p_kernel(
             )
             product_pass(h0_banks[i], 0, 1, piece)
             nc.scalar.copy(h[0][:, piece], h0_banks[i])
-        quantise_w(group_w(w_last[1], "grouped2", "words1", on_vector=True), 1, [1], "w_planes2")
         product_pass(h1_bank[:], 1, 1, slice(0, S))
         nc.scalar.copy(h[1][:], h1_bank[:])
+        last_turned = bank(7)
+        look_up_op(D - 1, "words1", last_turned)
+        last = held.tile([P, V_BLOCKS], F32, name="last")
+        for b in range(V_BLOCKS):
+            nc.scalar.activation(last[:, b : b + 1], last_turned[:, b * P + 24 : b * P + 25], COPY, scale=ct[:, 1, b, 1:2])
+        spread(7, [last[:, 0:1], last[:, 1:2]], 6)
 
         total = []
         for m in range(M_TILES):

@@ -48,7 +48,7 @@ def tile_picked_ysplat_none_p_kernel(
         w_raw = [held.tile([P, PACK, N], F32, name="w_raw%d" % o, tag="w_raw%d" % o, align_bytes=64) for o in range(PASSES)]
         ident = held.tile([P, P], F32, name="ident")
 
-        nc.gpsimd.memset(scales[32:64, :].bitcast(I32), 0)
+        nc.gpsimd.memset(scales[0:64, :].bitcast(I32), 0)
         nc.gpsimd.memset(scales[64:128, :].bitcast(I32), 0)
         make_identity(nc, ident[:])
         nc.vector.memset(op_t[32:64, :], 0.0)
@@ -81,13 +81,13 @@ def tile_picked_ysplat_none_p_kernel(
         load_fall()
         load_pos(0)
         load_pos(1)
-        nc.sync.dma_start(scales[0:32, :].bitcast(I32), x_scales.rearrange("o q c -> (o q) c").bitcast(I32))
+        nc.sync.dma_start(scales[12:44, :].bitcast(I32), x_scales.rearrange("o q c -> (o q) c").bitcast(I32))
         load_offs()
         load_words(0)
         load_pos(2)
-        load_pos(3)
         load_w(1)
         load_words(1)
+        load_pos(3)
 
         def turn(dst, src):
             for b in range(V_BLOCKS):
@@ -107,6 +107,7 @@ def tile_picked_ysplat_none_p_kernel(
         nc.vector.tensor_copy(x_rows[:], scales[:].indirect(offs_t[:]))
 
         x_codes = [held.tile([P, S], U32, name="x_codes0", align_bytes=64)]
+        plane_start = [12, 0]
         w_codes = {}
         w_planes = {}
 
@@ -135,28 +136,29 @@ def tile_picked_ysplat_none_p_kernel(
                 lhsT=w_codes[o, m].bitcast(FP8X4),
                 lhsT_scale=w_planes[o, m],
                 rhs=x_codes[o][:, cols].bitcast(FP8X4),
-                rhs_scale=x_planes[4 * o : P, cols],
+                rhs_scale=x_planes[plane_start[o] : P, cols],
                 start=(o == 0),
                 stop=(o == PASSES - 1),
             )
 
         grouped0 = group_w(w_raw[0], "grouped0", "grouped0")
-        x_planes = held.tile([P, S], U8, name="x_planes", tag="w_raw0", align_bytes=64)
-        nc.vector.tensor_copy(x_planes[:].bitcast(I32), x_rows[:].bitcast(I32))
-        for o in range(PASSES):
-            for q in range(4):
-                if o + q > 0:
-                    nc.scalar.dma_start(
-                        x_planes[32 * q + 4 * o : 32 * q + 4 * o + 4, :].bitcast(I32),
-                        x_rows[16 * o + 4 * q : 16 * o + 4 * q + 4, :].bitcast(I32),
-                    )
-        quantise_w(grouped0, 0, [0, 1], "w_planes0")
-        look_up_op(2, "a_rows2", turned[1][:, 0:V])
-
         pair = held.tile([P, 2, V_BLOCKS, 2], F32, name="pair")
         ct = held.tile([P, 2, V_BLOCKS, 2], F32, name="ct")
         step = P + 4
-        nc.scalar.copy(pair[:, :, :, 0].rearrange("p d b -> p (d b)"), turned[0][:, 0:512:step])
+        nc.vector.tensor_copy(pair[:, :, :, 0].rearrange("p d b -> p (d b)"), turned[0][:, 0:512:step])
+        quantise_w(grouped0, 0, [0, 1], "w_planes0")
+        x_planes = held.tile([P, S], U8, name="x_planes", tag="grouped0", align_bytes=64)
+        nc.vector.tensor_copy(x_planes[:].bitcast(I32), x_rows[:].bitcast(I32))
+        for o in range(PASSES):
+            for q in range(4):
+                source = 12 + 16 * o + 4 * q
+                target = 32 * q + plane_start[o]
+                if source != target:
+                    nc.scalar.dma_start(
+                        x_planes[target : target + 4, :].bitcast(I32), x_rows[source : source + 4, :].bitcast(I32)
+                    )
+        look_up_op(2, "a_rows2", turned[1][:, 0:V])
+
         nc.gpsimd.tensor_scalar(pair[:, :, :, 1], pair[:, :, :, 0], -1.0, 1.0, MULT, ADD)
         nc.gpsimd.tensor_tensor(ct[:, 0, :, :], pair[:, 1, :, :], pair[:, 0, :, 1:2].to_broadcast([P, V_BLOCKS, 2]), MULT)
 

@@ -43,9 +43,10 @@ def tile_picked_ysplat_none_p_kernel(
         pos = [pos1, pos2, pos3, pos4]
         op_t = held.tile([P, S], F32, name="op_t")
         fall_t = held.tile([P, V], F32, name="fall_t")
-        words = [held.tile([P, T], I32, name="words%d" % o, tag="words%d" % o, align_bytes=64) for o in range(PASSES)]
+        words = [held.tile([P, T], I32, name="words0", align_bytes=64)]
         scales = held.tile([P, T], U8, name="scales", tag="scales", align_bytes=64)
-        w_raw = [held.tile([P, PACK, N], F32, name="w_raw%d" % o, tag="w_raw%d" % o, align_bytes=64) for o in range(PASSES)]
+        w_raw = [held.tile([P, PACK, N], F32, name="w_raw0", align_bytes=64)]
+        w_last = [held.tile([P, PACK, P], F32, name="w_last0", align_bytes=64)]
         ident = held.tile([P, P], F32, name="ident")
 
         nc.gpsimd.memset(scales[0:64, :].bitcast(I32), 0)
@@ -63,6 +64,10 @@ def tile_picked_ysplat_none_p_kernel(
             rows = w1[o * 512 : (o + 1) * 512, :]
             q.dma_start(w_raw[o][:], rows.rearrange("(p j) n -> p j n", j=PACK))
 
+        def load_w_tile(m):
+            rows = w1[512:1024, m * P : (m + 1) * P]
+            nc.sync.dma_start(w_last[m][:], rows.rearrange("(p j) n -> p j n", j=PACK))
+
         def load_op(q=nc.sync):
             q.dma_start(op_t[0:ROWS, :], op[0:ROWS, :])
 
@@ -76,38 +81,47 @@ def tile_picked_ysplat_none_p_kernel(
         def load_offs():
             nc.sync.dma_start(offs_t[:], offs)
 
-        load_w(0)
+        load_w_tile(0)
+        load_offs()
+        nc.sync.dma_start(scales[12:44, :].bitcast(I32), x_scales.rearrange("o q c -> (o q) c").bitcast(I32))
+        load_pos(0)
         load_op()
         load_fall()
-        load_pos(0)
-        load_pos(1)
-        nc.sync.dma_start(scales[12:44, :].bitcast(I32), x_scales.rearrange("o q c -> (o q) c").bitcast(I32))
-        load_offs()
+        load_w(0)
+        for d in range(1, D):
+            load_pos(d)
         load_words(0)
-        load_pos(2)
-        load_w(1)
+
+        plane_start = [12, 0]
+        x_rows = held.tile([P, S], U8, name="x_rows", tag="x_rows", align_bytes=64)
+        x_planes = held.tile([P, S], U8, name="x_planes", align_bytes=64)
+        nc.gpsimd.memset(x_planes[64:128, :].bitcast(I32), 0)
+        nc.vector.tensor_copy(x_rows[:], scales[:].indirect(offs_t[:]))
+        nc.vector.tensor_copy(x_planes[0:64, :].bitcast(I32), x_rows[0:64, :].bitcast(I32))
+        for q in (3, 2, 1, 0):
+            for o in range(PASSES):
+                source = 12 + 16 * o + 4 * q
+                target = 32 * q + plane_start[o]
+                if source != target:
+                    nc.sync.dma_start(
+                        x_planes[target : target + 4, :].bitcast(I32), x_rows[source : source + 4, :].bitcast(I32)
+                    )
+        words.append(held.tile([P, T], I32, name="words1", tag="scales", align_bytes=64))
+        w_last.append(held.tile([P, PACK, P], F32, name="w_last1", tag="x_rows", align_bytes=64))
         load_words(1)
-        load_pos(3)
+        load_w_tile(1)
 
         def turn(dst, src):
             for b in range(V_BLOCKS):
                 nc.tensor.transpose(dst[:, b * P : (b + 1) * P], src[:, b * P : (b + 1) * P], ident[:])
 
         turned = [bank(0), bank(1)]
-
-        def look_up_op(d, tag, dst):
-            a_rows = held.tile([P, V], F32, name="a_rows%d" % d, tag=tag, align_bytes=64)
+        for d in range(D):
+            a_rows = held.tile([P, V], F32, name="a_rows%d" % d, tag="a_rows%d" % d, align_bytes=64)
             nc.vector.tensor_tensor(a_rows[:], op_t[:].indirect(pos_t[d][:]), fall_t[:], MULT)
-            turn(dst, a_rows)
+            turn(turned[d // 2][:, (d % 2) * V : (d % 2 + 1) * V], a_rows)
 
-
-        for d in range(2):
-            look_up_op(d, "a_rows%d" % d, turned[0][:, d * V : (d + 1) * V])
-        x_rows = held.tile([P, S], U8, name="x_rows", align_bytes=64)
-        nc.vector.tensor_copy(x_rows[:], scales[:].indirect(offs_t[:]))
-
-        x_codes = [held.tile([P, S], U32, name="x_codes0", align_bytes=64)]
-        plane_start = [12, 0]
+        x_codes = [held.tile([P, S], U32, name="x_codes%d" % o, align_bytes=64) for o in range(PASSES)]
         w_codes = {}
         w_planes = {}
 
@@ -141,46 +155,29 @@ def tile_picked_ysplat_none_p_kernel(
                 stop=(o == PASSES - 1),
             )
 
-        grouped0 = group_w(w_raw[0], "grouped0", "grouped0")
-        pair = held.tile([P, 2, V_BLOCKS, 2], F32, name="pair")
-        ct = held.tile([P, 2, V_BLOCKS, 2], F32, name="ct")
-        step = P + 4
-        nc.vector.tensor_copy(pair[:, :, :, 0].rearrange("p d b -> p (d b)"), turned[0][:, 0:512:step])
-        quantise_w(grouped0, 0, [0, 1], "w_planes0")
-        x_planes = held.tile([P, S], U8, name="x_planes", tag="grouped0", align_bytes=64)
-        nc.vector.tensor_copy(x_planes[:].bitcast(I32), x_rows[:].bitcast(I32))
-        for o in range(PASSES):
-            for q in range(4):
-                source = 12 + 16 * o + 4 * q
-                target = 32 * q + plane_start[o]
-                if source != target:
-                    nc.scalar.dma_start(
-                        x_planes[target : target + 4, :].bitcast(I32), x_rows[source : source + 4, :].bitcast(I32)
-                    )
-        look_up_op(2, "a_rows2", turned[1][:, 0:V])
+        quantise_w(group_w(w_last[0], "grouped1", "grouped1"), 1, [0], "w_planes1")
+        quantise_w(group_w(w_raw[0], "grouped0", "grouped0"), 0, [0, 1], "a_rows2")
 
-        nc.gpsimd.tensor_scalar(pair[:, :, :, 1], pair[:, :, :, 0], -1.0, 1.0, MULT, ADD)
-        nc.gpsimd.tensor_tensor(ct[:, 0, :, :], pair[:, 1, :, :], pair[:, 0, :, 1:2].to_broadcast([P, V_BLOCKS, 2]), MULT)
+        pair = held.tile([P, D, V_BLOCKS, 2], F32, name="pair")
+        ct = held.tile([P, D, V_BLOCKS, 2], F32, name="ct")
+        step = P + 4
+        nc.scalar.copy(pair[:, 0:2, :, 0].rearrange("p d b -> p (d b)"), turned[0][:, 0:512:step])
+        nc.gpsimd.tensor_scalar(pair[:, 0:2, :, 1], pair[:, 0:2, :, 0], -1.0, 1.0, MULT, ADD)
+        nc.gpsimd.tensor_tensor(ct[:, 1, :, :], pair[:, 1, :, :], pair[:, 0, :, 1:2].to_broadcast([P, V_BLOCKS, 2]), MULT)
+        nc.scalar.copy(pair[:, 2:4, :, 0].rearrange("p d b -> p (d b)"), turned[1][:, 16:512:step])
+        nc.gpsimd.tensor_scalar(pair[:, 2, :, 1], pair[:, 2, :, 0], -1.0, 1.0, MULT, ADD)
+        nc.gpsimd.tensor_tensor(ct[:, 2, :, :], pair[:, 2, :, :], ct[:, 1, :, 1:2].to_broadcast([P, V_BLOCKS, 2]), MULT)
+        nc.gpsimd.tensor_tensor(ct[:, 3, :, 0], pair[:, 3, :, 0], ct[:, 2, :, 1], MULT)
+        weight_rows = held.tile([P, D * V], F32, name="weight_rows")
+        for i in range(2):
+            spread_bank = bank(2 + i)
+            for c in range(4):
+                source = pair if (i == 0 and c < 2) else ct
+                column = source[:, 2 * i + c // 2, c % 2, 0:1]
+                nc.tensor.transpose(spread_bank[:, c * P : (c + 1) * P], column.to_broadcast([P, P]), ident[:])
+            nc.scalar.copy(weight_rows[:, i * 512 : (i + 1) * 512], spread_bank[:])
 
         nc.vector.tensor_copy(x_codes[0][:], words[0][:].bitcast(U32).indirect(offs_t[:]))
-        quantise_w(group_w(w_raw[1], "grouped1", "grouped1"), 1, [0, 1], "w_planes1")
-        x_codes.append(held.tile([P, S], U32, name="x_codes1", tag="grouped1", align_bytes=64))
-
-        late = held.tile([P, D * V + 2 * V_BLOCKS], F32, name="late", tag="w_raw1", align_bytes=64)
-        weight_rows = late[:, 0 : D * V]
-        third = late[:, D * V : D * V + 2 * V_BLOCKS].rearrange("p (b i) -> p b i", i=2)
-        nc.scalar.copy(third[:, :, 0], turned[1][:, 16:256:step])
-        nc.gpsimd.tensor_scalar(third[:, :, 1], third[:, :, 0], -1.0, 1.0, MULT, ADD)
-        nc.gpsimd.tensor_tensor(ct[:, 1, :, :], third, ct[:, 0, :, 1:2].to_broadcast([P, V_BLOCKS, 2]), MULT)
-
-        def spread(index, columns, first):
-            spread_bank = bank(index)
-            for c, column in enumerate(columns):
-                nc.tensor.transpose(spread_bank[:, c * P : (c + 1) * P], column.to_broadcast([P, P]), ident[:])
-            nc.scalar.copy(weight_rows[:, first * P : (first + len(columns)) * P], spread_bank[:, 0 : len(columns) * P])
-
-        spread(2, [pair[:, 0, 0, 0:1], pair[:, 0, 1, 0:1], ct[:, 0, 0, 0:1], ct[:, 0, 1, 0:1]], 0)
-        spread(3, [ct[:, 1, 0, 0:1], ct[:, 1, 1, 0:1]], 4)
 
         h = [held.tile([P, S], F32, name="h%d" % m) for m in range(M_TILES)]
         pieces = [slice(0, HALF), slice(HALF, S)]
@@ -195,14 +192,9 @@ def tile_picked_ysplat_none_p_kernel(
             )
             product_pass(h0_banks[i], 0, 1, piece)
             nc.scalar.copy(h[0][:, piece], h0_banks[i])
+        quantise_w(group_w(w_last[1], "grouped2", "scales", on_vector=True), 1, [1], "w_planes2")
         product_pass(h1_bank[:], 1, 1, slice(0, S))
         nc.scalar.copy(h[1][:], h1_bank[:])
-        last_turned = bank(7)
-        look_up_op(D - 1, "words1", last_turned)
-        last = held.tile([P, V_BLOCKS], F32, name="last")
-        for b in range(V_BLOCKS):
-            nc.scalar.activation(last[:, b : b + 1], last_turned[:, b * P + 24 : b * P + 25], COPY, scale=ct[:, 1, b, 1:2])
-        spread(7, [last[:, 0:1], last[:, 1:2]], 6)
 
         total = []
         for m in range(M_TILES):

@@ -5,12 +5,19 @@ from concourse.masks import make_identity
 
 K, T, S, V, N, D = 1024, 2048, 512, 256, 256, 4
 P = 128
+QUADRANT = 32
 PACK = 4
-PASSES = K // (P * PACK)
+K_PASS = P * PACK
+PASSES = K // K_PASS
 M_TILES = N // P
 V_BLOCKS = V // P
 HALF = S // 2
-ROWS = 32
+BANK = 512
+RUN = 4
+
+ROWS_AT = 12
+PLANE_START = (12, 0)
+GPSIMD_ZEROES = 1280
 
 FLOPS = 2 * K * N * S
 
@@ -36,7 +43,7 @@ def tile_picked_ysplat_none_p_kernel(
         psum = ctx.enter_context(tc.psum_pool(name="psum", bufs=1))
 
         def bank(index):
-            return psum.tile([P, 512], F32, name="bank%d" % index)
+            return psum.tile([P, BANK], F32, name="bank%d" % index)
 
         offs_t = held.tile([P, S // 16], U16, name="offs_t")
         pos_t = [held.tile([P, V // 16], U16, name="pos_t%d" % d) for d in range(D)]
@@ -45,95 +52,77 @@ def tile_picked_ysplat_none_p_kernel(
         fall_t = held.tile([P, V], F32, name="fall_t")
         words = [held.tile([P, T], I32, name="words0", align_bytes=64)]
         scales = held.tile([P, T], U8, name="scales", tag="scales", align_bytes=64)
-        w_raw = [held.tile([P, PACK, N], F32, name="w_raw0", align_bytes=64)]
+        w_first = held.tile([P, PACK, N], F32, name="w_raw0", align_bytes=64)
         w_last = [held.tile([P, PACK, P], F32, name="w_last0", align_bytes=64)]
         ident = held.tile([P, P], F32, name="ident")
 
-        nc.gpsimd.memset(scales[0:64, :].bitcast(I32), 0)
+        nc.gpsimd.memset(scales[0:64, 0:GPSIMD_ZEROES].bitcast(I32), 0)
+        nc.vector.memset(scales[0:64, GPSIMD_ZEROES:T].bitcast(I32), 0)
         nc.gpsimd.memset(scales[64:128, :].bitcast(I32), 0)
         make_identity(nc, ident[:])
-        nc.vector.memset(op_t[32:64, :], 0.0)
-        nc.vector.memset(op_t[64:128, :], 0.0)
-        nc.vector.memset(fall_t[32:64, :], 0.0)
-        nc.vector.memset(fall_t[64:128, :], 0.0)
+        for tile in (op_t, fall_t):
+            nc.vector.memset(tile[32:64, :], 0.0)
+            nc.vector.memset(tile[64:128, :], 0.0)
 
-        def load_words(o, q=nc.sync):
-            q.dma_start(words[o][:], x_words[o].rearrange("p c r -> p (c r)").bitcast(I32))
+        def load_words(o):
+            nc.sync.dma_start(words[o][:], x_words[o].rearrange("p c r -> p (c r)").bitcast(I32))
 
-        def load_w(o, q=nc.sync):
-            rows = w1[o * 512 : (o + 1) * 512, :]
-            q.dma_start(w_raw[o][:], rows.rearrange("(p j) n -> p j n", j=PACK))
+        def load_w(dst, o, cols):
+            rows = w1[o * K_PASS : (o + 1) * K_PASS, cols]
+            nc.sync.dma_start(dst[:], rows.rearrange("(p j) n -> p j n", j=PACK))
 
-        def load_w_tile(m):
-            rows = w1[512:1024, m * P : (m + 1) * P]
-            nc.sync.dma_start(w_last[m][:], rows.rearrange("(p j) n -> p j n", j=PACK))
-
-        def load_op(q=nc.sync):
-            q.dma_start(op_t[0:ROWS, :], op[0:ROWS, :])
-
-        def load_fall(q=nc.sync):
-            fall_rows = fall.rearrange("d p v -> (d p) v")
-            q.dma_start(fall_t[0:ROWS, :], fall_rows[0 : D * P : D * P // ROWS, :])
-
-        def load_pos(d):
-            nc.sync.dma_start(pos_t[d][:], pos[d])
-
-        def load_offs():
-            nc.sync.dma_start(offs_t[:], offs)
-
-        load_w_tile(0)
-        load_offs()
-        nc.sync.dma_start(scales[12:44, :].bitcast(I32), x_scales.rearrange("o q c -> (o q) c").bitcast(I32))
-        load_pos(0)
-        load_op()
-        load_fall()
-        load_w(0)
+        load_w(w_last[0], 1, slice(0, P))
+        nc.sync.dma_start(offs_t[:], offs)
+        nc.sync.dma_start(
+            scales[ROWS_AT : ROWS_AT + 32, :].bitcast(I32), x_scales.rearrange("o q c -> (o q) c").bitcast(I32)
+        )
+        nc.sync.dma_start(pos_t[0][:], pos[0])
+        nc.sync.dma_start(op_t[0:QUADRANT, :], op[0:QUADRANT, :])
+        fall_rows = fall.rearrange("d p v -> (d p) v")
+        nc.sync.dma_start(fall_t[0:QUADRANT, :], fall_rows[0 : D * P : D * P // QUADRANT, :])
+        load_w(w_first, 0, slice(0, N))
         for d in range(1, D):
-            load_pos(d)
+            nc.sync.dma_start(pos_t[d][:], pos[d])
         load_words(0)
 
-        plane_start = [12, 0]
         x_rows = held.tile([P, S], U8, name="x_rows", tag="x_rows", align_bytes=64)
         x_planes = held.tile([P, S], U8, name="x_planes", align_bytes=64)
         nc.gpsimd.memset(x_planes[64:128, :].bitcast(I32), 0)
         nc.vector.tensor_copy(x_rows[:], scales[:].indirect(offs_t[:]))
         nc.vector.tensor_copy(x_planes[0:64, :].bitcast(I32), x_rows[0:64, :].bitcast(I32))
-        for q in (3, 2, 1, 0):
+        for q in reversed(range(P // QUADRANT)):
             for o in range(PASSES):
-                source = 12 + 16 * o + 4 * q
-                target = 32 * q + plane_start[o]
+                source = ROWS_AT + 16 * o + 4 * q
+                target = QUADRANT * q + PLANE_START[o]
                 if source != target:
                     nc.sync.dma_start(
                         x_planes[target : target + 4, :].bitcast(I32), x_rows[source : source + 4, :].bitcast(I32)
                     )
+
         words.append(held.tile([P, T], I32, name="words1", tag="scales", align_bytes=64))
         w_last.append(held.tile([P, PACK, P], F32, name="w_last1", tag="x_rows", align_bytes=64))
         load_words(1)
-        load_w_tile(1)
-
-        def turn(dst, src):
-            for b in range(V_BLOCKS):
-                nc.tensor.transpose(dst[:, b * P : (b + 1) * P], src[:, b * P : (b + 1) * P], ident[:])
+        load_w(w_last[1], 1, slice(P, N))
 
         turned = [bank(0), bank(1)]
         for d in range(D):
             a_rows = held.tile([P, V], F32, name="a_rows%d" % d, tag="a_rows%d" % d, align_bytes=64)
             nc.vector.tensor_tensor(a_rows[:], op_t[:].indirect(pos_t[d][:]), fall_t[:], MULT)
-            turn(turned[d // 2][:, (d % 2) * V : (d % 2 + 1) * V], a_rows)
+            for b in range(V_BLOCKS):
+                first = (d % 2) * V + b * P
+                nc.tensor.transpose(turned[d // 2][:, first : first + P], a_rows[:, b * P : (b + 1) * P], ident[:])
 
         x_codes = [held.tile([P, S], U32, name="x_codes%d" % o, align_bytes=64) for o in range(PASSES)]
         w_codes = {}
         w_planes = {}
 
-        def group_w(raw, name, tag, on_vector=False):
+        def group_w(raw, name, tag, copy):
             grouped = held.tile([P, raw.shape[2], PACK], BF16, name=name, tag=tag, align_bytes=64)
-            dst = grouped[:].rearrange("p (c i) j -> p c j i", i=4)
-            src = raw[:].rearrange("p j (c i) -> p c j i", i=4)
-            if on_vector:
-                nc.vector.tensor_copy(dst, src)
-            else:
-                nc.scalar.activation(dst, src, COPY)
+            copy(grouped[:].rearrange("p (c i) j -> p c j i", i=RUN), raw[:].rearrange("p j (c i) -> p c j i", i=RUN))
             return grouped
+
+        def scalar_cast(dst, src):
+            nc.scalar.activation(dst, src, COPY)
 
         def quantise_w(grouped, o, tiles, tag):
             width = len(tiles) * P
@@ -150,58 +139,65 @@ def tile_picked_ysplat_none_p_kernel(
                 lhsT=w_codes[o, m].bitcast(FP8X4),
                 lhsT_scale=w_planes[o, m],
                 rhs=x_codes[o][:, cols].bitcast(FP8X4),
-                rhs_scale=x_planes[plane_start[o] : P, cols],
+                rhs_scale=x_planes[PLANE_START[o] : P, cols],
                 start=(o == 0),
                 stop=(o == PASSES - 1),
             )
 
-        quantise_w(group_w(w_last[0], "grouped1", "grouped1"), 1, [0], "w_planes1")
-        quantise_w(group_w(w_raw[0], "grouped0", "grouped0"), 0, [0, 1], "a_rows2")
+        quantise_w(group_w(w_last[0], "grouped1", "grouped1", scalar_cast), 1, [0], "w_planes1")
+        quantise_w(group_w(w_first, "grouped0", "grouped0", scalar_cast), 0, [0, 1], "a_rows2")
 
         pair = held.tile([P, D, V_BLOCKS, 2], F32, name="pair")
         ct = held.tile([P, D, V_BLOCKS, 2], F32, name="ct")
         step = P + 4
-        nc.scalar.copy(pair[:, 0:2, :, 0].rearrange("p d b -> p (d b)"), turned[0][:, 0:512:step])
+        both = [P, V_BLOCKS, 2]
+        nc.scalar.copy(pair[:, 0:2, :, 0].rearrange("p d b -> p (d b)"), turned[0][:, 0:BANK:step])
         nc.gpsimd.tensor_scalar(pair[:, 0:2, :, 1], pair[:, 0:2, :, 0], -1.0, 1.0, MULT, ADD)
-        nc.gpsimd.tensor_tensor(ct[:, 1, :, :], pair[:, 1, :, :], pair[:, 0, :, 1:2].to_broadcast([P, V_BLOCKS, 2]), MULT)
-        nc.scalar.copy(pair[:, 2:4, :, 0].rearrange("p d b -> p (d b)"), turned[1][:, 16:512:step])
+        nc.gpsimd.tensor_tensor(ct[:, 1, :, :], pair[:, 1, :, :], pair[:, 0, :, 1:2].to_broadcast(both), MULT)
+        nc.scalar.copy(pair[:, 2:4, :, 0].rearrange("p d b -> p (d b)"), turned[1][:, 16:BANK:step])
         nc.gpsimd.tensor_scalar(pair[:, 2, :, 1], pair[:, 2, :, 0], -1.0, 1.0, MULT, ADD)
-        nc.gpsimd.tensor_tensor(ct[:, 2, :, :], pair[:, 2, :, :], ct[:, 1, :, 1:2].to_broadcast([P, V_BLOCKS, 2]), MULT)
+        nc.gpsimd.tensor_tensor(ct[:, 2, :, :], pair[:, 2, :, :], ct[:, 1, :, 1:2].to_broadcast(both), MULT)
         nc.gpsimd.tensor_tensor(ct[:, 3, :, 0], pair[:, 3, :, 0], ct[:, 2, :, 1], MULT)
+
         weight_rows = held.tile([P, D * V], F32, name="weight_rows")
-        for i in range(2):
+        for i in range(D // 2):
             spread_bank = bank(2 + i)
-            for c in range(4):
-                source = pair if (i == 0 and c < 2) else ct
-                column = source[:, 2 * i + c // 2, c % 2, 0:1]
-                nc.tensor.transpose(spread_bank[:, c * P : (c + 1) * P], column.to_broadcast([P, P]), ident[:])
-            nc.scalar.copy(weight_rows[:, i * 512 : (i + 1) * 512], spread_bank[:])
+            for d in (2 * i, 2 * i + 1):
+                for b in range(V_BLOCKS):
+                    column = (pair if d == 0 else ct)[:, d, b, 0:1]
+                    first = (d % 2) * V + b * P
+                    nc.tensor.transpose(spread_bank[:, first : first + P], column.to_broadcast([P, P]), ident[:])
+            nc.scalar.copy(weight_rows[:, i * BANK : (i + 1) * BANK], spread_bank[:])
 
         nc.vector.tensor_copy(x_codes[0][:], words[0][:].bitcast(U32).indirect(offs_t[:]))
 
         h = [held.tile([P, S], F32, name="h%d" % m) for m in range(M_TILES)]
-        pieces = [slice(0, HALF), slice(HALF, S)]
-        h0_banks = [bank(4 + i)[:, 0 : piece.stop - piece.start] for i, piece in enumerate(pieces)]
+        halves = [slice(0, HALF), slice(HALF, S)]
+        h0_banks = [bank(4 + i)[:, 0:HALF] for i in range(2)]
         h1_bank = bank(6)
-        for i, piece in enumerate(pieces):
-            product_pass(h0_banks[i], 0, 0, piece)
+        for i, half in enumerate(halves):
+            product_pass(h0_banks[i], 0, 0, half)
         product_pass(h1_bank[:], 1, 0, slice(0, S))
-        for i, piece in enumerate(pieces):
+        for i, half in enumerate(halves):
             nc.vector.tensor_copy(
-                x_codes[1][:, piece], words[1][:].bitcast(U32).indirect(offs_t[:, piece.start // 16 : piece.stop // 16])
+                x_codes[1][:, half], words[1][:].bitcast(U32).indirect(offs_t[:, half.start // 16 : half.stop // 16])
             )
-            product_pass(h0_banks[i], 0, 1, piece)
-            nc.scalar.copy(h[0][:, piece], h0_banks[i])
-        quantise_w(group_w(w_last[1], "grouped2", "scales", on_vector=True), 1, [1], "w_planes2")
+            product_pass(h0_banks[i], 0, 1, half)
+            nc.scalar.copy(h[0][:, half], h0_banks[i])
+        quantise_w(group_w(w_last[1], "grouped2", "scales", nc.vector.tensor_copy), 1, [1], "w_planes2")
         product_pass(h1_bank[:], 1, 1, slice(0, S))
         nc.scalar.copy(h[1][:], h1_bank[:])
+
+        def weighted(m, d):
+            picked = ring.tile([P, V], F32, name="picked")
+            nc.vector.tensor_tensor(picked[:], h[m][:].indirect(pos_t[d][:]), weight_rows[:, d * V : (d + 1) * V], MULT)
+            return picked
 
         total = []
         for m in range(M_TILES):
             sum_banks = [bank(4 * m + b) for b in range(V_BLOCKS)]
             for d in range(D - 1):
-                picked = ring.tile([P, V], F32, name="picked")
-                nc.vector.tensor_tensor(picked[:], h[m][:].indirect(pos_t[d][:]), weight_rows[:, d * V : (d + 1) * V], MULT)
+                picked = weighted(m, d)
                 for b in range(V_BLOCKS):
                     nc.tensor.matmul(
                         sum_banks[b][:, 0:P], picked[:, b * P : (b + 1) * P], ident[:], is_transpose=True,
@@ -212,12 +208,9 @@ def tile_picked_ysplat_none_p_kernel(
                 summed = held.tile([P, P], F32, name="summed%d_%d" % (m, b))
                 nc.scalar.copy(summed[:], sum_banks[b][:, 0:P])
                 nc.tensor.transpose(total[m][:, b * P : (b + 1) * P], summed[:], ident[:])
-        back = []
-        for m in range(M_TILES):
-            picked = ring.tile([P, V], F32, name="picked")
-            nc.vector.tensor_tensor(picked[:], h[m][:].indirect(pos_t[D - 1][:]), weight_rows[:, (D - 1) * V : D * V], MULT)
-            back.append(picked)
+
+        fourth = [weighted(m, D - 1) for m in range(M_TILES)]
         for m, cols in [(0, slice(0, V)), (1, slice(0, P)), (1, slice(P, V))]:
             result = ring.tile([P, cols.stop - cols.start], F32, name="result")
-            nc.vector.tensor_tensor(result[:], total[m][:, cols], back[m][:, cols], ADD)
+            nc.vector.tensor_tensor(result[:], total[m][:, cols], fourth[m][:, cols], ADD)
             nc.sync.dma_start(out[m * P : (m + 1) * P, cols], result[:])

@@ -15,9 +15,9 @@ HALF = S // 2
 BANK = 512
 RUN = 4
 
-ROWS_AT = 12
+ROWS_AT = 96
 PLANE_START = (12, 0)
-GPSIMD_ZEROES = 1280
+LIVE_AT = P - 2 * D
 
 FLOPS = 2 * K * N * S
 
@@ -40,6 +40,7 @@ def tile_picked_ysplat_none_p_kernel(
     with ExitStack() as ctx:
         held = ctx.enter_context(tc.tile_pool(name="held", bufs=1))
         ring = ctx.enter_context(tc.tile_pool(name="ring", bufs=3))
+        placed = ctx.enter_context(tc.tile_pool(name="placed", bufs=1))
         psum = ctx.enter_context(tc.psum_pool(name="psum", bufs=1))
 
         def bank(index):
@@ -50,19 +51,20 @@ def tile_picked_ysplat_none_p_kernel(
         pos = [pos1, pos2, pos3, pos4]
         op_t = held.tile([P, S], F32, name="op_t")
         fall_t = held.tile([P, V], F32, name="fall_t")
-        words = [held.tile([P, T], I32, name="words0", align_bytes=64)]
-        scales = held.tile([P, T], U8, name="scales", tag="scales", align_bytes=64)
-        w_first = held.tile([P, PACK, N], F32, name="w_raw0", align_bytes=64)
-        w_last = [held.tile([P, PACK, P], F32, name="w_last0", align_bytes=64)]
+        words = [placed.tile([P, T], I32, name="words0", align_bytes=64, offset=16384)]
+        scales = placed.tile([P, T], U8, name="scales", align_bytes=64, offset=8128)
+        w_first = held.tile([P, PACK, N], F32, name="w_raw0", tag="w_raw0", align_bytes=64)
+        w_last = [placed.tile([P, PACK, P], F32, name="w_last0", align_bytes=64, offset=28672)]
         ident = held.tile([P, P], F32, name="ident")
+        x_rows = held.tile([P, S], U8, name="x_rows", align_bytes=64)
+        x_planes = [held.tile([P, S], U8, name="x_planes%d" % o, align_bytes=64) for o in range(PASSES)]
 
-        nc.gpsimd.memset(scales[0:64, 0:GPSIMD_ZEROES].bitcast(I32), 0)
-        nc.vector.memset(scales[0:64, GPSIMD_ZEROES:T].bitcast(I32), 0)
-        nc.gpsimd.memset(scales[64:128, :].bitcast(I32), 0)
-        make_identity(nc, ident[:])
+        nc.vector.memset(scales[0:ROWS_AT, :].bitcast(I32), 0)
         for tile in (op_t, fall_t):
-            nc.vector.memset(tile[32:64, :], 0.0)
-            nc.vector.memset(tile[64:128, :], 0.0)
+            nc.vector.memset(tile[0:LIVE_AT, :], 0.0)
+        make_identity(nc, ident[:])
+        for o in range(PASSES):
+            nc.gpsimd.memset(x_planes[o][:].bitcast(I32), 0)
 
         def load_words(o):
             nc.sync.dma_start(words[o][:], x_words[o].rearrange("p c r -> p (c r)").bitcast(I32))
@@ -71,64 +73,66 @@ def tile_picked_ysplat_none_p_kernel(
             rows = w1[o * K_PASS : (o + 1) * K_PASS, cols]
             nc.sync.dma_start(dst[:], rows.rearrange("(p j) n -> p j n", j=PACK))
 
-        load_w(w_last[0], 1, slice(0, P))
-        nc.sync.dma_start(offs_t[:], offs)
+        fall_rows = fall.rearrange("d p v -> (d p) v")
         nc.sync.dma_start(
             scales[ROWS_AT : ROWS_AT + 32, :].bitcast(I32), x_scales.rearrange("o q c -> (o q) c").bitcast(I32)
         )
-        nc.sync.dma_start(pos_t[0][:], pos[0])
-        nc.sync.dma_start(op_t[0:QUADRANT, :], op[0:QUADRANT, :])
-        fall_rows = fall.rearrange("d p v -> (d p) v")
-        nc.sync.dma_start(fall_t[0:QUADRANT, :], fall_rows[0 : D * P : D * P // QUADRANT, :])
+        nc.sync.dma_start(offs_t[:], offs)
         load_w(w_first, 0, slice(0, N))
-        for d in range(1, D):
-            nc.sync.dma_start(pos_t[d][:], pos[d])
+        nc.sync.dma_start(op_t[LIVE_AT:P, :], op[LIVE_AT:P, :])
+        nc.sync.dma_start(fall_t[LIVE_AT:P, :], fall_rows[0 : D * P : P // 2, :])
+        nc.sync.dma_start(pos_t[1][:], pos[1])
+        nc.sync.dma_start(pos_t[2][:], pos[2])
         load_words(0)
+        nc.sync.dma_start(pos_t[3][:], pos[3])
+        nc.sync.dma_start(pos_t[0][:], pos[0])
+        load_w(w_last[0], 1, slice(0, P))
 
-        x_rows = held.tile([P, S], U8, name="x_rows", tag="x_rows", align_bytes=64)
-        x_planes = held.tile([P, S], U8, name="x_planes", align_bytes=64)
-        nc.gpsimd.memset(x_planes[64:128, :].bitcast(I32), 0)
         nc.vector.tensor_copy(x_rows[:], scales[:].indirect(offs_t[:]))
-        nc.vector.tensor_copy(x_planes[0:64, :].bitcast(I32), x_rows[0:64, :].bitcast(I32))
-        for q in reversed(range(P // QUADRANT)):
-            for o in range(PASSES):
+
+        def place_scales(o):
+            for q in range(P // QUADRANT):
                 source = ROWS_AT + 16 * o + 4 * q
                 target = QUADRANT * q + PLANE_START[o]
-                if source != target:
+                if source == target:
+                    rows = slice(QUADRANT * q, QUADRANT * (q + 1))
+                    nc.vector.tensor_copy(x_planes[o][rows, :].bitcast(I32), x_rows[rows, :].bitcast(I32))
+                else:
                     nc.sync.dma_start(
-                        x_planes[target : target + 4, :].bitcast(I32), x_rows[source : source + 4, :].bitcast(I32)
+                        x_planes[o][target : target + 4, :].bitcast(I32), x_rows[source : source + 4, :].bitcast(I32)
                     )
 
-        words.append(held.tile([P, T], I32, name="words1", tag="scales", align_bytes=64))
-        w_last.append(held.tile([P, PACK, P], F32, name="w_last1", tag="x_rows", align_bytes=64))
+        place_scales(0)
+        words.append(placed.tile([P, T], I32, name="words1", align_bytes=64, offset=0))
         load_words(1)
+        place_scales(1)
+        w_last.append(placed.tile([P, PACK, P], F32, name="w_last1", align_bytes=64, offset=10112))
         load_w(w_last[1], 1, slice(P, N))
 
-        turned = [bank(0), bank(1)]
-        for d in range(D):
-            a_rows = held.tile([P, V], F32, name="a_rows%d" % d, tag="a_rows%d" % d, align_bytes=64)
+        def look_up(d):
+            a_rows = placed.tile([P, V], F32, name="a_rows%d" % d, align_bytes=64, offset=(24576, 25600, 24576, 16384)[d])
             nc.vector.tensor_tensor(a_rows[:], op_t[:].indirect(pos_t[d][:]), fall_t[:], MULT)
+            return a_rows
+
+        def turn(a_rows, acc, first):
             for b in range(V_BLOCKS):
-                first = (d % 2) * V + b * P
-                nc.tensor.transpose(turned[d // 2][:, first : first + P], a_rows[:, b * P : (b + 1) * P], ident[:])
+                nc.tensor.transpose(acc[:, first + b * P : first + (b + 1) * P], a_rows[:, b * P : (b + 1) * P], ident[:])
 
         x_codes = [held.tile([P, S], U32, name="x_codes%d" % o, align_bytes=64) for o in range(PASSES)]
         w_codes = {}
         w_planes = {}
 
-        def group_w(raw, name, tag, copy):
-            grouped = held.tile([P, raw.shape[2], PACK], BF16, name=name, tag=tag, align_bytes=64)
-            copy(grouped[:].rearrange("p (c i) j -> p c j i", i=RUN), raw[:].rearrange("p j (c i) -> p c j i", i=RUN))
+        def group_w(raw, grouped, copy):
+            copy(grouped[:, :, :].rearrange("p (c i) j -> p c j i", i=RUN), raw[:].rearrange("p j (c i) -> p c j i", i=RUN))
             return grouped
 
         def scalar_cast(dst, src):
             nc.scalar.activation(dst, src, COPY)
 
-        def quantise_w(grouped, o, tiles, tag):
+        def quantise_w(grouped, o, tiles, codes):
             width = len(tiles) * P
-            codes = held.tile([P, width], U32, name="w_codes%d_%d" % (o, tiles[0]), align_bytes=64)
-            planes = held.tile([P, width], U8, name="w_planes%d_%d" % (o, tiles[0]), tag=tag, align_bytes=64)
-            nc.vector.quantize_mx(out=codes[:].bitcast(FP8X4), scales=planes[:], in_=grouped[:].rearrange("p n j -> p (n j)"))
+            planes = held.tile([P, width], U8, name="w_planes%d_%d" % (o, tiles[0]), align_bytes=64)
+            nc.vector.quantize_mx(out=codes[:].bitcast(FP8X4), scales=planes[:], in_=grouped[:, :, :].rearrange("p n j -> p (n j)"))
             for i, m in enumerate(tiles):
                 w_codes[o, m] = codes[:, i * P : (i + 1) * P]
                 w_planes[o, m] = planes[:, i * P : (i + 1) * P]
@@ -139,78 +143,103 @@ def tile_picked_ysplat_none_p_kernel(
                 lhsT=w_codes[o, m].bitcast(FP8X4),
                 lhsT_scale=w_planes[o, m],
                 rhs=x_codes[o][:, cols].bitcast(FP8X4),
-                rhs_scale=x_planes[PLANE_START[o] : P, cols],
+                rhs_scale=x_planes[o][PLANE_START[o] : P, cols],
                 start=(o == 0),
                 stop=(o == PASSES - 1),
             )
 
-        quantise_w(group_w(w_last[0], "grouped1", "grouped1", scalar_cast), 1, [0], "w_planes1")
-        quantise_w(group_w(w_first, "grouped0", "grouped0", scalar_cast), 0, [0, 1], "a_rows2")
+        weight_rows = {}
 
-        pair = held.tile([P, D, V_BLOCKS, 2], F32, name="pair")
-        ct = held.tile([P, D, V_BLOCKS, 2], F32, name="ct")
-        step = P + 4
-        both = [P, V_BLOCKS, 2]
-        nc.scalar.copy(pair[:, 0:2, :, 0].rearrange("p d b -> p (d b)"), turned[0][:, 0:BANK:step])
-        nc.gpsimd.tensor_scalar(pair[:, 0:2, :, 1], pair[:, 0:2, :, 0], -1.0, 1.0, MULT, ADD)
-        nc.gpsimd.tensor_tensor(ct[:, 1, :, :], pair[:, 1, :, :], pair[:, 0, :, 1:2].to_broadcast(both), MULT)
-        nc.scalar.copy(pair[:, 2:4, :, 0].rearrange("p d b -> p (d b)"), turned[1][:, 16:BANK:step])
-        nc.gpsimd.tensor_scalar(pair[:, 2, :, 1], pair[:, 2, :, 0], -1.0, 1.0, MULT, ADD)
-        nc.gpsimd.tensor_tensor(ct[:, 2, :, :], pair[:, 2, :, :], ct[:, 1, :, 1:2].to_broadcast(both), MULT)
-        nc.gpsimd.tensor_tensor(ct[:, 3, :, 0], pair[:, 3, :, 0], ct[:, 2, :, 1], MULT)
-
-        weight_rows = held.tile([P, D * V], F32, name="weight_rows")
-        for i in range(D // 2):
-            spread_bank = bank(2 + i)
-            for d in (2 * i, 2 * i + 1):
+        def spread(acc, columns):
+            first_d = columns[0][0]
+            rows = placed.tile(
+                [P, len(columns) * V], F32, name="weight_rows%d" % first_d, align_bytes=64, offset={1: 28672 + 64, 3: 32768, 0: 33792}[first_d]
+            )
+            for i, (d, column) in enumerate(columns):
                 for b in range(V_BLOCKS):
-                    column = (pair if d == 0 else ct)[:, d, b, 0:1]
-                    first = (d % 2) * V + b * P
-                    nc.tensor.transpose(spread_bank[:, first : first + P], column.to_broadcast([P, P]), ident[:])
-            nc.scalar.copy(weight_rows[:, i * BANK : (i + 1) * BANK], spread_bank[:])
+                    first = i * V + b * P
+                    nc.tensor.transpose(acc[:, first : first + P], column[:, b : b + 1].to_broadcast([P, P]), ident[:])
+                weight_rows[d] = rows[:, i * V : (i + 1) * V]
+            nc.scalar.copy(rows[:], acc[:, 0 : len(columns) * V])
 
+        second = held.tile([P, V_BLOCKS, 2], F32, name="second")
+        a_front = held.tile([P, V_BLOCKS], F32, name="a_front")
+        through = held.tile([P, V_BLOCKS], F32, name="through")
+
+        grouped0 = group_w(w_first, held.tile([P, N, PACK], BF16, name="grouped0", align_bytes=64), scalar_cast)
+        turned = bank(0)
+        turn(look_up(1), turned, 0)
+        turn(look_up(2), turned, V)
+        quantise_w(grouped0, 0, [0, 1], held.tile([P, N], U32, name="w_codes0", align_bytes=64))
+        pair = held.tile([P, 2, V_BLOCKS, 2], F32, name="pair", tag="w_raw0", align_bytes=64)
+        step = P + 1
+        picks = turned[:, LIVE_AT + 2 : BANK : step]
+        nc.scalar.copy(pair[:, :, :, 0].rearrange("p d b -> p (d b)"), picks)
+        nc.scalar.activation(pair[:, :, :, 1].rearrange("p d b -> p (d b)"), picks, COPY, bias=1.0, scale=-1.0)
+        nc.gpsimd.tensor_tensor(second[:], pair[:, 1, :, :], pair[:, 0, :, 1:2].to_broadcast([P, V_BLOCKS, 2]), MULT)
+        grouped1 = group_w(w_last[0], placed.tile([P, P, PACK], BF16, name="grouped1", align_bytes=64, offset=24576), scalar_cast)
+        spread(bank(3), [(1, pair[:, 0, :, 0]), (2, second[:, :, 0])])
         nc.vector.tensor_copy(x_codes[0][:], words[0][:].bitcast(U32).indirect(offs_t[:]))
+        turned = bank(1)
+        turn(look_up(3), turned, 0)
+        quantise_w(grouped1, 1, [0], placed.tile([P, P], U32, name="w_codes10", align_bytes=64, offset=16384 + 1024))
+        third = placed.tile([P, V_BLOCKS], F32, name="third", align_bytes=64, offset=28672)
+        for b in range(V_BLOCKS):
+            column = b * P + LIVE_AT + 6
+            nc.scalar.activation(third[:, b : b + 1], turned[:, column : column + 1], COPY, scale=second[:, b, 1:2])
 
         h = [held.tile([P, S], F32, name="h%d" % m) for m in range(M_TILES)]
         halves = [slice(0, HALF), slice(HALF, S)]
-        h0_banks = [bank(4 + i)[:, 0:HALF] for i in range(2)]
+        h0_banks = [bank(index)[:, 0:HALF] for index in (5, 1)]
         h1_bank = bank(6)
-        for i, half in enumerate(halves):
-            product_pass(h0_banks[i], 0, 0, half)
+        product_pass(h0_banks[0], 0, 0, halves[0])
         product_pass(h1_bank[:], 1, 0, slice(0, S))
+        product_pass(h0_banks[1], 0, 0, halves[1])
+        front_rows = look_up(0)
         for i, half in enumerate(halves):
             nc.vector.tensor_copy(
                 x_codes[1][:, half], words[1][:].bitcast(U32).indirect(offs_t[:, half.start // 16 : half.stop // 16])
             )
             product_pass(h0_banks[i], 0, 1, half)
             nc.scalar.copy(h[0][:, half], h0_banks[i])
-        quantise_w(group_w(w_last[1], "grouped2", "scales", nc.vector.tensor_copy), 1, [1], "w_planes2")
+        spread(bank(5), [(3, third)])
+        grouped2 = group_w(w_last[1], placed.tile([P, N, PACK], BF16, name="grouped2", align_bytes=64, offset=64)[:, 0:P, :], nc.vector.tensor_copy)
+        quantise_w(grouped2, 1, [1], held.tile([P, P], U32, name="w_codes11", align_bytes=64))
         product_pass(h1_bank[:], 1, 1, slice(0, S))
         nc.scalar.copy(h[1][:], h1_bank[:])
+        turned = bank(6)
+        turn(front_rows, turned, 0)
+        nc.scalar.copy(a_front[:], turned[:, LIVE_AT:V:P])
+        nc.scalar.activation(through[:], turned[:, LIVE_AT:V:P], COPY, bias=1.0, scale=-1.0)
 
         def weighted(m, d):
-            picked = ring.tile([P, V], F32, name="picked")
-            nc.vector.tensor_tensor(picked[:], h[m][:].indirect(pos_t[d][:]), weight_rows[:, d * V : (d + 1) * V], MULT)
+            if m == 0 and d > 0:
+                picked = placed.tile([P, V], F32, name="picked_first%d" % d, align_bytes=64, offset=1024 * (d - 1))
+            else:
+                picked = ring.tile([P, V], F32, name="picked")
+            nc.vector.tensor_tensor(picked[:], h[m][:].indirect(pos_t[d][:]), weight_rows[d], MULT)
             return picked
 
         total = []
         for m in range(M_TILES):
-            sum_banks = [bank(4 * m + b) for b in range(V_BLOCKS)]
-            for d in range(D - 1):
+            sum_banks = [bank(2 - 2 * m + b) for b in range(V_BLOCKS)]
+            for d in range(1, D):
                 picked = weighted(m, d)
                 for b in range(V_BLOCKS):
                     nc.tensor.matmul(
                         sum_banks[b][:, 0:P], picked[:, b * P : (b + 1) * P], ident[:], is_transpose=True,
-                        start=(d == 0), stop=(d == D - 2),
+                        start=(d == 1), stop=(d == D - 1),
                     )
-            total.append(bank(2 + m))
+            if m == 0:
+                spread(bank(4), [(0, a_front)])
+            total.append(bank(7 - 2 * m))
             for b in range(V_BLOCKS):
                 summed = held.tile([P, P], F32, name="summed%d_%d" % (m, b))
-                nc.scalar.copy(summed[:], sum_banks[b][:, 0:P])
+                nc.scalar.activation(summed[:], sum_banks[b][:, 0:P], COPY, scale=through[:, b : b + 1])
                 nc.tensor.transpose(total[m][:, b * P : (b + 1) * P], summed[:], ident[:])
 
-        fourth = [weighted(m, D - 1) for m in range(M_TILES)]
+        front = [weighted(m, 0) for m in range(M_TILES)]
         for m, cols in [(0, slice(0, V)), (1, slice(0, P)), (1, slice(P, V))]:
             result = ring.tile([P, cols.stop - cols.start], F32, name="result")
-            nc.vector.tensor_tensor(result[:], total[m][:, cols], fourth[m][:, cols], ADD)
+            nc.vector.tensor_tensor(result[:], total[m][:, cols], front[m][:, cols], ADD)
             nc.sync.dma_start(out[m * P : (m + 1) * P, cols], result[:])

@@ -110,7 +110,7 @@ def tile_picked_ysplat_none_p_kernel(
         load_w(w_last[1], 1, slice(P, N))
 
         def look_up(d):
-            a_rows = placed.tile([P, V], F32, name="a_rows%d" % d, align_bytes=64, offset=(24576, 25600, 24576, 16384)[d])
+            a_rows = placed.tile([P, V], F32, name="a_rows%d" % d, align_bytes=64, offset=(4096, 25600, 24576, 16384)[d])
             nc.vector.tensor_tensor(a_rows[:], op_t[:].indirect(pos_t[d][:]), fall_t[:], MULT)
             return a_rows
 
@@ -162,7 +162,7 @@ def tile_picked_ysplat_none_p_kernel(
                 weight_rows[d] = rows[:, i * V : (i + 1) * V]
             nc.scalar.copy(rows[:], acc[:, 0 : len(columns) * V])
 
-        second = held.tile([P, V_BLOCKS, 2], F32, name="second")
+        second = placed.tile([P, V_BLOCKS, 2], F32, name="second", align_bytes=64, offset=36864 + 64)
         a_front = held.tile([P, V_BLOCKS], F32, name="a_front")
         through = held.tile([P, V_BLOCKS], F32, name="through")
 
@@ -176,7 +176,8 @@ def tile_picked_ysplat_none_p_kernel(
         picks = turned[:, LIVE_AT + 2 : BANK : step]
         nc.scalar.copy(pair[:, :, :, 0].rearrange("p d b -> p (d b)"), picks)
         nc.scalar.activation(pair[:, :, :, 1].rearrange("p d b -> p (d b)"), picks, COPY, bias=1.0, scale=-1.0)
-        nc.gpsimd.tensor_tensor(second[:], pair[:, 1, :, :], pair[:, 0, :, 1:2].to_broadcast([P, V_BLOCKS, 2]), MULT)
+        for b in range(V_BLOCKS):
+            nc.scalar.activation(second[:, b, :], pair[:, 1, b, :], COPY, scale=pair[:, 0, b, 1:2])
         grouped1 = group_w(w_last[0], placed.tile([P, P, PACK], BF16, name="grouped1", align_bytes=64, offset=24576), scalar_cast)
         spread(bank(3), [(1, pair[:, 0, :, 0]), (2, second[:, :, 0])])
         nc.vector.tensor_copy(x_codes[0][:], words[0][:].bitcast(U32).indirect(offs_t[:]))
@@ -188,14 +189,14 @@ def tile_picked_ysplat_none_p_kernel(
             column = b * P + LIVE_AT + 6
             nc.scalar.activation(third[:, b : b + 1], turned[:, column : column + 1], COPY, scale=second[:, b, 1:2])
 
-        h = [held.tile([P, S], F32, name="h%d" % m) for m in range(M_TILES)]
+        grouped2 = group_w(w_last[1], placed.tile([P, N, PACK], BF16, name="grouped2", align_bytes=64, offset=36864 + 64)[:, 0:P, :], scalar_cast)
+        h = [placed.tile([P, S], F32, name="h0", align_bytes=64, offset=10112 + 64), held.tile([P, S], F32, name="h1")]
         halves = [slice(0, HALF), slice(HALF, S)]
         h0_banks = [bank(index)[:, 0:HALF] for index in (5, 1)]
         h1_bank = bank(6)
         product_pass(h0_banks[0], 0, 0, halves[0])
         product_pass(h1_bank[:], 1, 0, slice(0, S))
         product_pass(h0_banks[1], 0, 0, halves[1])
-        front_rows = look_up(0)
         for i, half in enumerate(halves):
             nc.vector.tensor_copy(
                 x_codes[1][:, half], words[1][:].bitcast(U32).indirect(offs_t[:, half.start // 16 : half.stop // 16])
@@ -203,8 +204,8 @@ def tile_picked_ysplat_none_p_kernel(
             product_pass(h0_banks[i], 0, 1, half)
             nc.scalar.copy(h[0][:, half], h0_banks[i])
         spread(bank(5), [(3, third)])
-        grouped2 = group_w(w_last[1], placed.tile([P, N, PACK], BF16, name="grouped2", align_bytes=64, offset=64)[:, 0:P, :], nc.vector.tensor_copy)
-        quantise_w(grouped2, 1, [1], held.tile([P, P], U32, name="w_codes11", align_bytes=64))
+        front_rows = look_up(0)
+        quantise_w(grouped2, 1, [1], placed.tile([P, P], U32, name="w_codes11", align_bytes=64, offset=6144))
         product_pass(h1_bank[:], 1, 1, slice(0, S))
         nc.scalar.copy(h[1][:], h1_bank[:])
         turned = bank(6)
@@ -214,7 +215,7 @@ def tile_picked_ysplat_none_p_kernel(
 
         def weighted(m, d):
             if m == 0 and d > 0:
-                picked = placed.tile([P, V], F32, name="picked_first%d" % d, align_bytes=64, offset=1024 * (d - 1))
+                picked = placed.tile([P, V], F32, name="picked_first%d" % d, align_bytes=64, offset=36864 + 1024 * (d - 1))
             else:
                 picked = ring.tile([P, V], F32, name="picked")
             nc.vector.tensor_tensor(picked[:], h[m][:].indirect(pos_t[d][:]), weight_rows[d], MULT)

@@ -9,15 +9,39 @@ QUADRANT = 32
 PACK = 4
 K_PASS = P * PACK
 PASSES = K // K_PASS
-M_TILES = N // P
+PLANE_ROWS = K_PASS // 32
 V_BLOCKS = V // P
 HALF = S // 2
 BANK = 512
 RUN = 4
 
-ROWS_AT = 96
+ROWS_AT = P - PASSES * PLANE_ROWS
 PLANE_START = (12, 0)
-LIVE_AT = P - 2 * D
+OP_ROW = P - 1
+FALL_ROW = P - D
+
+KIB = 1024
+LINK = 64
+ROW_BYTES = 4 * V
+WORDS1_AT = 0
+SCALES_AT = WORDS1_AT + 4 * T - LINK
+W_LAST1_AT = SCALES_AT + T - LINK
+H0_AT = W_LAST1_AT + LINK
+FOURTH_AT = WORDS1_AT + 4 * KIB
+CODES11_AT = WORDS1_AT + 6 * KIB
+WORDS0_AT = 16 * KIB
+THIRD_AT = WORDS0_AT
+CODES10_AT = WORDS0_AT + 6 * KIB
+OP_ROWS0_AT = 26 * KIB
+OP_ROWS2_AT = OP_ROWS0_AT - ROW_BYTES + LINK
+GROUPED01_AT = OP_ROWS0_AT + ROW_BYTES - LINK
+OP_ROWS1_AT = 30 * KIB
+BEHIND0_AT = 31 * KIB
+W_FIRST_AT = 40 * KIB
+GROUPED10_AT = W_FIRST_AT + 2 * KIB
+W_LAST0_AT = 48 * KIB
+OP_AT = 52 * KIB
+SECOND_ROWS_AT = OP_AT + ROW_BYTES
 
 FLOPS = 2 * K * N * S
 
@@ -31,6 +55,7 @@ FP8X4 = mybir.dt.float8_e4m3fn_x4
 COPY = mybir.ActivationFunctionType.Copy
 MULT = mybir.AluOpType.mult
 ADD = mybir.AluOpType.add
+SUBTRACT = mybir.AluOpType.subtract
 
 
 def tile_picked_ysplat_none_p_kernel(
@@ -39,30 +64,32 @@ def tile_picked_ysplat_none_p_kernel(
     nc = tc.nc
     with ExitStack() as ctx:
         held = ctx.enter_context(tc.tile_pool(name="held", bufs=1))
-        ring = ctx.enter_context(tc.tile_pool(name="ring", bufs=3))
         placed = ctx.enter_context(tc.tile_pool(name="placed", bufs=1))
         psum = ctx.enter_context(tc.psum_pool(name="psum", bufs=1))
 
         def bank(index):
             return psum.tile([P, BANK], F32, name="bank%d" % index)
 
+        def place(shape, dtype, name, offset):
+            return placed.tile(shape, dtype, name=name, align_bytes=LINK, offset=offset)
+
         offs_t = held.tile([P, S // 16], U16, name="offs_t")
         pos_t = [held.tile([P, V // 16], U16, name="pos_t%d" % d) for d in range(D)]
         pos = [pos1, pos2, pos3, pos4]
-        op_t = held.tile([P, S], F32, name="op_t")
+        op_t = place([P, S], F32, "op_t", OP_AT)
         fall_t = held.tile([P, V], F32, name="fall_t")
-        words = [placed.tile([P, T], I32, name="words0", align_bytes=64, offset=16384)]
-        scales = placed.tile([P, T], U8, name="scales", align_bytes=64, offset=8128)
-        w_first = held.tile([P, PACK, N], F32, name="w_raw0", tag="w_raw0", align_bytes=64)
-        w_last = [placed.tile([P, PACK, P], F32, name="w_last0", align_bytes=64, offset=28672)]
+        words = [place([P, T], I32, "words0", WORDS0_AT)]
+        scales = place([P, T], U8, "scales", SCALES_AT)
+        w_first = place([P, PACK, N], F32, "w_raw0", W_FIRST_AT)
+        w_last = [place([P, PACK, P], F32, "w_last0", W_LAST0_AT)]
         ident = held.tile([P, P], F32, name="ident")
         x_rows = held.tile([P, S], U8, name="x_rows", align_bytes=64)
         x_planes = [held.tile([P, S], U8, name="x_planes%d" % o, align_bytes=64) for o in range(PASSES)]
 
+        nc.vector.memset(op_t[0:OP_ROW, :], 0.0)
         nc.vector.memset(scales[0:ROWS_AT, :].bitcast(I32), 0)
-        for tile in (op_t, fall_t):
-            nc.vector.memset(tile[0:LIVE_AT, :], 0.0)
         make_identity(nc, ident[:])
+        nc.scalar.activation(fall_t[0:FALL_ROW, :], op_t[0:FALL_ROW, 0:V], COPY)
         for o in range(PASSES):
             nc.gpsimd.memset(x_planes[o][:].bitcast(I32), 0)
 
@@ -73,26 +100,23 @@ def tile_picked_ysplat_none_p_kernel(
             rows = w1[o * K_PASS : (o + 1) * K_PASS, cols]
             nc.sync.dma_start(dst[:], rows.rearrange("(p j) n -> p j n", j=PACK))
 
-        fall_rows = fall.rearrange("d p v -> (d p) v")
-        nc.sync.dma_start(
-            scales[ROWS_AT : ROWS_AT + 32, :].bitcast(I32), x_scales.rearrange("o q c -> (o q) c").bitcast(I32)
-        )
+        nc.sync.dma_start(scales[ROWS_AT:P, :].bitcast(I32), x_scales.rearrange("o q c -> (o q) c").bitcast(I32))
         nc.sync.dma_start(offs_t[:], offs)
-        load_w(w_first, 0, slice(0, N))
-        nc.sync.dma_start(op_t[LIVE_AT:P, :], op[LIVE_AT:P, :])
-        nc.sync.dma_start(fall_t[LIVE_AT:P, :], fall_rows[0 : D * P : P // 2, :])
-        nc.sync.dma_start(pos_t[1][:], pos[1])
-        nc.sync.dma_start(pos_t[2][:], pos[2])
-        load_words(0)
-        nc.sync.dma_start(pos_t[3][:], pos[3])
+        nc.scalar.dma_start(op_t[OP_ROW:P, :], op[0:1, :])
         nc.sync.dma_start(pos_t[0][:], pos[0])
+        load_w(w_first, 0, slice(0, N))
+        nc.scalar.dma_start(fall_t[FALL_ROW:P, :], fall[:, 0, :])
+        nc.sync.dma_start(pos_t[1][:], pos[1])
+        load_words(0)
+        nc.sync.dma_start(pos_t[2][:], pos[2])
+        nc.sync.dma_start(pos_t[3][:], pos[3])
         load_w(w_last[0], 1, slice(0, P))
 
         nc.vector.tensor_copy(x_rows[:], scales[:].indirect(offs_t[:]))
 
         def place_scales(o):
             for q in range(P // QUADRANT):
-                source = ROWS_AT + 16 * o + 4 * q
+                source = ROWS_AT + PLANE_ROWS * o + 4 * q
                 target = QUADRANT * q + PLANE_START[o]
                 if source == target:
                     rows = slice(QUADRANT * q, QUADRANT * (q + 1))
@@ -103,144 +127,191 @@ def tile_picked_ysplat_none_p_kernel(
                     )
 
         place_scales(0)
-        words.append(placed.tile([P, T], I32, name="words1", align_bytes=64, offset=0))
+        words.append(place([P, T], I32, "words1", WORDS1_AT))
         load_words(1)
-        place_scales(1)
-        w_last.append(placed.tile([P, PACK, P], F32, name="w_last1", align_bytes=64, offset=10112))
+        w_last.append(place([P, PACK, P], F32, "w_last1", W_LAST1_AT))
         load_w(w_last[1], 1, slice(P, N))
+        place_scales(1)
 
-        def look_up(d):
-            a_rows = placed.tile([P, V], F32, name="a_rows%d" % d, align_bytes=64, offset=(4096, 25600, 24576, 16384)[d])
-            nc.vector.tensor_tensor(a_rows[:], op_t[:].indirect(pos_t[d][:]), fall_t[:], MULT)
-            return a_rows
-
-        def turn(a_rows, acc, first):
-            for b in range(V_BLOCKS):
-                nc.tensor.transpose(acc[:, first + b * P : first + (b + 1) * P], a_rows[:, b * P : (b + 1) * P], ident[:])
-
-        x_codes = [held.tile([P, S], U32, name="x_codes%d" % o, align_bytes=64) for o in range(PASSES)]
+        x_codes = []
         w_codes = {}
         w_planes = {}
 
         def group_w(raw, grouped, copy):
-            copy(grouped[:, :, :].rearrange("p (c i) j -> p c j i", i=RUN), raw[:].rearrange("p j (c i) -> p c j i", i=RUN))
+            copy(grouped[:].rearrange("p (c i) j -> p c j i", i=RUN), raw.rearrange("p j (c i) -> p c j i", i=RUN))
             return grouped
 
-        def scalar_cast(dst, src):
+        def scalar_copy(dst, src):
             nc.scalar.activation(dst, src, COPY)
 
-        def quantise_w(grouped, o, tiles, codes):
-            width = len(tiles) * P
-            planes = held.tile([P, width], U8, name="w_planes%d_%d" % (o, tiles[0]), align_bytes=64)
-            nc.vector.quantize_mx(out=codes[:].bitcast(FP8X4), scales=planes[:], in_=grouped[:, :, :].rearrange("p n j -> p (n j)"))
-            for i, m in enumerate(tiles):
-                w_codes[o, m] = codes[:, i * P : (i + 1) * P]
-                w_planes[o, m] = planes[:, i * P : (i + 1) * P]
+        def quantise_w(grouped, o, m, codes):
+            plane = held.tile([P, P], U8, name="w_planes%d_%d" % (o, m), align_bytes=64)
+            nc.vector.quantize_mx(
+                out=codes[:].bitcast(FP8X4), scales=plane[:], in_=grouped[:].rearrange("p n j -> p (n j)")
+            )
+            w_codes[o, m] = codes
+            w_planes[o, m] = plane
 
         def product_pass(acc, m, o, cols):
             nc.tensor.matmul_mx(
                 out=acc,
-                lhsT=w_codes[o, m].bitcast(FP8X4),
-                lhsT_scale=w_planes[o, m],
+                lhsT=w_codes[o, m][:].bitcast(FP8X4),
+                lhsT_scale=w_planes[o, m][:],
                 rhs=x_codes[o][:, cols].bitcast(FP8X4),
                 rhs_scale=x_planes[o][PLANE_START[o] : P, cols],
                 start=(o == 0),
                 stop=(o == PASSES - 1),
             )
 
-        weight_rows = {}
+        def turn(rows, acc):
+            for b in range(V_BLOCKS):
+                nc.tensor.transpose(acc[:, b * P : (b + 1) * P], rows[:, b * P : (b + 1) * P], ident[:])
 
-        def spread(acc, columns):
-            first_d = columns[0][0]
-            rows = placed.tile(
-                [P, len(columns) * V], F32, name="weight_rows%d" % first_d, align_bytes=64, offset={1: 28672 + 64, 3: 32768, 0: 33792}[first_d]
-            )
-            for i, (d, column) in enumerate(columns):
+        def look_up(d, offset, acc):
+            op_rows = place([P, V], F32, "op_rows%d" % d, offset)
+            scalar_copy(op_rows[:], op_t[:].indirect(pos_t[d][:]))
+            turn(op_rows, acc)
+            return acc[:, OP_ROW:V:P]
+
+        def spread(acc, weights):
+            for i, weight in enumerate(weights):
                 for b in range(V_BLOCKS):
                     first = i * V + b * P
-                    nc.tensor.transpose(acc[:, first : first + P], column[:, b : b + 1].to_broadcast([P, P]), ident[:])
-                weight_rows[d] = rows[:, i * V : (i + 1) * V]
-            nc.scalar.copy(rows[:], acc[:, 0 : len(columns) * V])
+                    nc.tensor.transpose(acc[:, first : first + P], weight[:, b : b + 1].to_broadcast([P, P]), ident[:])
 
-        second = placed.tile([P, V_BLOCKS, 2], F32, name="second", align_bytes=64, offset=36864 + 64)
-        a_front = held.tile([P, V_BLOCKS], F32, name="a_front")
-        through = held.tile([P, V_BLOCKS], F32, name="through")
+        def twice(values):
+            return values.unsqueeze(1).to_broadcast([P, 2, V_BLOCKS])
 
-        grouped0 = group_w(w_first, held.tile([P, N, PACK], BF16, name="grouped0", align_bytes=64), scalar_cast)
-        turned = bank(0)
-        turn(look_up(1), turned, 0)
-        turn(look_up(2), turned, V)
-        quantise_w(grouped0, 0, [0, 1], held.tile([P, N], U32, name="w_codes0", align_bytes=64))
-        pair = held.tile([P, 2, V_BLOCKS, 2], F32, name="pair", tag="w_raw0", align_bytes=64)
-        step = P + 1
-        picks = turned[:, LIVE_AT + 2 : BANK : step]
-        nc.scalar.copy(pair[:, :, :, 0].rearrange("p d b -> p (d b)"), picks)
-        nc.scalar.activation(pair[:, :, :, 1].rearrange("p d b -> p (d b)"), picks, COPY, bias=1.0, scale=-1.0)
-        for b in range(V_BLOCKS):
-            nc.scalar.activation(second[:, b, :], pair[:, 1, b, :], COPY, scale=pair[:, 0, b, 1:2])
-        grouped1 = group_w(w_last[0], placed.tile([P, P, PACK], BF16, name="grouped1", align_bytes=64, offset=24576), scalar_cast)
-        spread(bank(3), [(1, pair[:, 0, :, 0]), (2, second[:, :, 0])])
+        chain = held.tile([P, D + 2, V_BLOCKS], F32, name="chain")
+        minus_fall = chain[:, 0:D, :]
+        behind1 = chain[:, D : D + 2, :]
+        fall_bank = bank(0)
+        turn(fall_t, fall_bank)
+        opacity_banks = [bank(1), bank(2)]
+        opacity0 = look_up(0, OP_ROWS0_AT, opacity_banks[0])
+        opacity1 = look_up(1, OP_ROWS1_AT, opacity_banks[1])
+        nc.scalar.activation(
+            minus_fall, fall_bank[:, 0:V].rearrange("p (b c) -> p c b", b=V_BLOCKS)[:, FALL_ROW:P, :], COPY, scale=-1.0
+        )
+
+        grouped00 = held.tile([P, P, PACK], BF16, name="grouped00", align_bytes=64)
+        group_w(w_first[:, :, 0:P], grouped00, nc.vector.tensor_copy)
+        grouped01 = group_w(w_first[:, :, P:N], place([P, P, PACK], BF16, "grouped01", GROUPED01_AT), scalar_copy)
+        quantise_w(grouped00, 0, 0, held.tile([P, P], U32, name="w_codes00", align_bytes=64))
+        first_w = held.tile([P, V_BLOCKS], F32, name="first_w")
+        nc.vector.tensor_tensor(first_w[:], opacity0, minus_fall[:, 0, :], MULT)
+        behind0 = place([P, 2, V_BLOCKS], F32, "behind0", BEHIND0_AT)
+        nc.vector.scalar_tensor_tensor(behind0[:], twice(first_w[:]), 1.0, minus_fall[:, 2:D, :], ADD, MULT)
+        minus_a1 = held.tile([P, V_BLOCKS], F32, name="minus_a1")
+        nc.vector.tensor_tensor(minus_a1[:], opacity1, minus_fall[:, 1, :], MULT)
+        second_w = held.tile([P, V_BLOCKS], F32, name="second_w")
+        nc.vector.scalar_tensor_tensor(second_w[:], first_w[:], 1.0, minus_a1[:], ADD, MULT)
+        nc.vector.scalar_tensor_tensor(behind1, twice(minus_a1[:]), 1.0, behind0[:], ADD, MULT)
+        quantise_w(grouped01, 0, 1, held.tile([P, P], U32, name="w_codes01", align_bytes=64))
+        near_banks = [bank(1), bank(2)]
+        spread(near_banks[0], [first_w])
+        spread(near_banks[1], [second_w])
+        opacity2 = look_up(2, OP_ROWS2_AT, bank(6))
+        grouped10 = group_w(w_last[0][:], place([P, P, PACK], BF16, "grouped10", GROUPED10_AT), scalar_copy)
+        opacity3 = look_up(3, W_LAST0_AT, bank(7))
+
+        x_codes.append(place([P, S], U32, "x_codes0", BEHIND0_AT))
         nc.vector.tensor_copy(x_codes[0][:], words[0][:].bitcast(U32).indirect(offs_t[:]))
-        turned = bank(1)
-        turn(look_up(3), turned, 0)
-        quantise_w(grouped1, 1, [0], placed.tile([P, P], U32, name="w_codes10", align_bytes=64, offset=16384 + 1024))
-        third = placed.tile([P, V_BLOCKS], F32, name="third", align_bytes=64, offset=28672)
-        for b in range(V_BLOCKS):
-            column = b * P + LIVE_AT + 6
-            nc.scalar.activation(third[:, b : b + 1], turned[:, column : column + 1], COPY, scale=second[:, b, 1:2])
+        second_rows = place([P, V], F32, "second_rows", SECOND_ROWS_AT)
+        nc.scalar.copy(second_rows[:], near_banks[1][:, 0:V])
+        third = place([P, 2, V_BLOCKS], F32, "third", THIRD_AT)
+        nc.vector.tensor_tensor(third[:], twice(opacity2), chain[:, 2 : D + 1 : 2, :], MULT)
+        behind2 = held.tile([P, V_BLOCKS], F32, name="behind2")
+        nc.vector.scalar_tensor_tensor(behind2[:], third[:, 0, :], 1.0, behind1[:, 1, :], ADD, MULT)
+        quantise_w(grouped10, 1, 0, place([P, P], U32, "w_codes10", CODES10_AT))
+        grouped11 = group_w(w_last[1][:], place([P, P, PACK], BF16, "grouped11", OP_AT), scalar_copy)
+        x_codes.append(place([P, S], U32, "x_codes1", GROUPED10_AT))
 
-        grouped2 = group_w(w_last[1], placed.tile([P, N, PACK], BF16, name="grouped2", align_bytes=64, offset=36864 + 64)[:, 0:P, :], scalar_cast)
-        h = [placed.tile([P, S], F32, name="h0", align_bytes=64, offset=10112 + 64), held.tile([P, S], F32, name="h1")]
+        h = [place([P, S], F32, "h0", H0_AT), held.tile([P, S], F32, name="h1")]
         halves = [slice(0, HALF), slice(HALF, S)]
-        h0_banks = [bank(index)[:, 0:HALF] for index in (5, 1)]
-        h1_bank = bank(6)
-        product_pass(h0_banks[0], 0, 0, halves[0])
-        product_pass(h1_bank[:], 1, 0, slice(0, S))
-        product_pass(h0_banks[1], 0, 0, halves[1])
+        h0_pieces = [slice(0, HALF), slice(HALF, HALF + P), slice(HALF + P, S)]
+        h0_banks = [bank(index)[:, 0 : cols.stop - cols.start] for index, cols in zip((4, 5, 0), h0_pieces)]
+        h1_banks = [bank(index)[:, 0:HALF] for index in (6, 3)]
+        for i, cols in enumerate(h0_pieces):
+            product_pass(h0_banks[i], 0, 0, cols)
         for i, half in enumerate(halves):
+            product_pass(h1_banks[i], 1, 0, half)
+        for i, cols in enumerate(h0_pieces):
             nc.vector.tensor_copy(
-                x_codes[1][:, half], words[1][:].bitcast(U32).indirect(offs_t[:, half.start // 16 : half.stop // 16])
+                x_codes[1][:, cols], words[1][:].bitcast(U32).indirect(offs_t[:, cols.start // 16 : cols.stop // 16])
             )
-            product_pass(h0_banks[i], 0, 1, half)
-            nc.scalar.copy(h[0][:, half], h0_banks[i])
-        spread(bank(5), [(3, third)])
-        front_rows = look_up(0)
-        quantise_w(grouped2, 1, [1], placed.tile([P, P], U32, name="w_codes11", align_bytes=64, offset=6144))
-        product_pass(h1_bank[:], 1, 1, slice(0, S))
-        nc.scalar.copy(h[1][:], h1_bank[:])
-        turned = bank(6)
-        turn(front_rows, turned, 0)
-        nc.scalar.copy(a_front[:], turned[:, LIVE_AT:V:P])
-        nc.scalar.activation(through[:], turned[:, LIVE_AT:V:P], COPY, bias=1.0, scale=-1.0)
+            product_pass(h0_banks[i], 0, 1, cols)
+            nc.scalar.copy(h[0][:, cols], h0_banks[i])
+        fourth = place([P, V_BLOCKS], F32, "fourth", FOURTH_AT)
+        nc.vector.tensor_tensor(fourth[:], opacity3, behind2[:], MULT)
+        quantise_w(grouped11, 1, 1, place([P, P], U32, "w_codes11", CODES11_AT))
+        first_rows = place([P, V], F32, "first_rows", OP_AT)
+        nc.vector.tensor_copy(first_rows[:], near_banks[0][:, 0:V])
+        near_rows = [first_rows, second_rows]
+        for i, half in enumerate(halves):
+            product_pass(h1_banks[i], 1, 1, half)
+            nc.scalar.copy(h[1][:, half], h1_banks[i])
+        far_bank = bank(6)
+        spread(far_bank, [third[:, 1, :], fourth])
 
-        def weighted(m, d):
-            if m == 0 and d > 0:
-                picked = placed.tile([P, V], F32, name="picked_first%d" % d, align_bytes=64, offset=36864 + 1024 * (d - 1))
-            else:
-                picked = ring.tile([P, V], F32, name="picked")
-            nc.vector.tensor_tensor(picked[:], h[m][:].indirect(pos_t[d][:]), weight_rows[d], MULT)
-            return picked
+        def weighted(m, d, tag):
+            product = held.tile([P, V], F32, name="product%d_%d" % (m, d), tag=tag)
+            nc.vector.tensor_tensor(product[:], h[m][:].indirect(pos_t[d][:]), near_rows[d][:], MULT)
+            return product
 
-        total = []
-        for m in range(M_TILES):
-            sum_banks = [bank(2 - 2 * m + b) for b in range(V_BLOCKS)]
-            for d in range(1, D):
-                picked = weighted(m, d)
-                for b in range(V_BLOCKS):
-                    nc.tensor.matmul(
-                        sum_banks[b][:, 0:P], picked[:, b * P : (b + 1) * P], ident[:], is_transpose=True,
-                        start=(d == 1), stop=(d == D - 1),
-                    )
-            if m == 0:
-                spread(bank(4), [(0, a_front)])
-            total.append(bank(7 - 2 * m))
-            for b in range(V_BLOCKS):
-                summed = held.tile([P, P], F32, name="summed%d_%d" % (m, b))
-                nc.scalar.activation(summed[:], sum_banks[b][:, 0:P], COPY, scale=through[:, b : b + 1])
-                nc.tensor.transpose(total[m][:, b * P : (b + 1) * P], summed[:], ident[:])
+        def picked(m, d, columns):
+            scalar_copy(columns[:], h[m][:].indirect(pos_t[d][:]))
+            return columns
 
-        front = [weighted(m, 0) for m in range(M_TILES)]
-        for m, cols in [(0, slice(0, V)), (1, slice(0, P)), (1, slice(P, V))]:
-            result = ring.tile([P, cols.stop - cols.start], F32, name="result")
-            nc.vector.tensor_tensor(result[:], total[m][:, cols], front[m][:, cols], ADD)
+        def tagged(name, tag):
+            return held.tile([P, V], F32, name=name, tag=tag)
+
+        def times(columns, m, d, cols):
+            product = held.tile([P, cols.stop - cols.start], F32, name="product%d_%d_%d" % (m, d, cols.start))
+            first = (d - 2) * V
+            nc.vector.tensor_tensor(product[:], columns[:, cols], far_bank[:, first + cols.start : first + cols.stop], MULT)
+            return product
+
+        def add_turned(acc, block, start, stop):
+            nc.tensor.matmul(acc, block, ident[:], is_transpose=True, start=start, stop=stop)
+
+        whole = slice(0, V)
+        blocks = [slice(b * P, (b + 1) * P) for b in range(V_BLOCKS)]
+        sum0 = bank(1)
+        sum1 = [bank(2)[:, 0:P], bank(4)[:, 0:P]]
+        total0 = bank(0)
+        total1 = [bank(3)[:, 0:P], bank(7)[:, 0:P]]
+
+        def add0(product, start, stop):
+            for b, cols in enumerate(blocks):
+                add_turned(sum0[:, cols], product[:, cols], start and b == 0, stop and b == V_BLOCKS - 1)
+
+        def add1(product, start):
+            for b, cols in enumerate(blocks):
+                add_turned(sum1[b], product[:, cols], start, False)
+
+        add0(weighted(0, 1, "p01"), True, False)
+        columns02 = picked(0, 2, place([P, V], F32, "columns0_2", CODES11_AT))
+        add0(weighted(0, 0, "p00"), False, False)
+        columns12 = picked(1, 2, tagged("columns1_2", "c12"))
+        columns13 = picked(1, 3, tagged("columns1_3", "c13"))
+        add1(weighted(1, 0, "p10"), True)
+        add0(times(columns02, 0, 2, whole), False, True)
+        add1(times(columns12, 1, 2, whole), False)
+        for b, cols in enumerate(blocks):
+            add_turned(sum1[b], times(columns13, 1, 3, cols)[:], False, True)
+        columns03 = picked(0, 3, tagged("columns0_3", "p10"))
+        summed0 = held.tile([P, V], F32, name="summed0")
+        nc.scalar.activation(summed0[:], sum0[:, whole], COPY, scale=-1.0)
+        turn(summed0, total0)
+        last1 = weighted(1, 1, "c12")
+        for b in range(V_BLOCKS):
+            summed1 = held.tile([P, P], F32, name="summed1_%d" % b)
+            nc.scalar.activation(summed1[:], sum1[b], COPY, scale=-1.0)
+            nc.tensor.transpose(total1[b], summed1[:], ident[:])
+        last0 = times(columns03, 0, 3, whole)
+        results = [(0, whole, total0[:, whole], last0)] + [(1, blocks[b], total1[b], last1) for b in range(V_BLOCKS)]
+        for m, cols, total, last in results:
+            result = held.tile([P, cols.stop - cols.start], F32, name="result%d_%d" % (m, cols.start))
+            nc.vector.tensor_tensor(result[:], total, last[:, cols], SUBTRACT)
             nc.sync.dma_start(out[m * P : (m + 1) * P, cols], result[:])

@@ -23,25 +23,16 @@ FALL_ROW = P - D
 KIB = 1024
 LINK = 64
 ROW_BYTES = 4 * V
-WORDS1_AT = 0
+WORDS0_AT = 0
+GROUPED10_AT = WORDS0_AT
+WORDS1_AT = 8 * KIB
 SCALES_AT = WORDS1_AT + 4 * T - LINK
-W_LAST1_AT = SCALES_AT + T - LINK
-H0_AT = W_LAST1_AT + LINK
-FOURTH_AT = WORDS1_AT + 4 * KIB
-CODES11_AT = WORDS1_AT + 6 * KIB
-WORDS0_AT = 16 * KIB
-THIRD_AT = WORDS0_AT
-CODES10_AT = WORDS0_AT + 6 * KIB
-OP_ROWS0_AT = 26 * KIB
-OP_ROWS2_AT = OP_ROWS0_AT - ROW_BYTES + LINK
-GROUPED01_AT = OP_ROWS0_AT + ROW_BYTES - LINK
-OP_ROWS1_AT = 30 * KIB
-BEHIND0_AT = 31 * KIB
-W_FIRST_AT = 40 * KIB
-GROUPED10_AT = W_FIRST_AT + 2 * KIB
-W_LAST0_AT = 48 * KIB
-OP_AT = 52 * KIB
-SECOND_ROWS_AT = OP_AT + ROW_BYTES
+W_FIRST_AT = 20 * KIB
+OP_AT = 24 * KIB
+BEHIND0_AT = 28 * KIB
+H0_AT = 32 * KIB
+CODES11_AT = 36 * KIB
+OP_ROWS0_AT = 38 * KIB
 
 FLOPS = 2 * K * N * S
 
@@ -80,8 +71,7 @@ def tile_picked_ysplat_none_p_kernel(
         fall_t = held.tile([P, V], F32, name="fall_t")
         words = [place([P, T], I32, "words0", WORDS0_AT)]
         scales = place([P, T], U8, "scales", SCALES_AT)
-        w_first = place([P, PACK, N], F32, "w_raw0", W_FIRST_AT)
-        w_last = [place([P, PACK, P], F32, "w_last0", W_LAST0_AT)]
+        w_raw = [place([P, PACK, N], F32, "w_raw0", W_FIRST_AT), held.tile([P, PACK, N], F32, name="w_raw1")]
         ident = held.tile([P, P], F32, name="ident")
         x_rows = held.tile([P, S], U8, name="x_rows", align_bytes=64)
         x_planes = [held.tile([P, S], U8, name="x_planes%d" % o, align_bytes=64) for o in range(PASSES)]
@@ -96,21 +86,21 @@ def tile_picked_ysplat_none_p_kernel(
         def load_words(o):
             nc.sync.dma_start(words[o][:], x_words[o].rearrange("p c r -> p (c r)").bitcast(I32))
 
-        def load_w(dst, o, cols):
-            rows = w1[o * K_PASS : (o + 1) * K_PASS, cols]
-            nc.sync.dma_start(dst[:], rows.rearrange("(p j) n -> p j n", j=PACK))
+        def load_w(o):
+            rows = w1[o * K_PASS : (o + 1) * K_PASS, :]
+            nc.sync.dma_start(w_raw[o][:], rows.rearrange("(p j) n -> p j n", j=PACK))
 
         nc.sync.dma_start(scales[ROWS_AT:P, :].bitcast(I32), x_scales.rearrange("o q c -> (o q) c").bitcast(I32))
         nc.sync.dma_start(offs_t[:], offs)
         nc.scalar.dma_start(op_t[OP_ROW:P, :], op[0:1, :])
         nc.sync.dma_start(pos_t[0][:], pos[0])
-        load_w(w_first, 0, slice(0, N))
+        load_w(0)
         nc.scalar.dma_start(fall_t[FALL_ROW:P, :], fall[:, 0, :])
         nc.sync.dma_start(pos_t[1][:], pos[1])
         load_words(0)
         nc.sync.dma_start(pos_t[2][:], pos[2])
         nc.sync.dma_start(pos_t[3][:], pos[3])
-        load_w(w_last[0], 1, slice(0, P))
+        load_w(1)
 
         nc.vector.tensor_copy(x_rows[:], scales[:].indirect(offs_t[:]))
 
@@ -129,15 +119,15 @@ def tile_picked_ysplat_none_p_kernel(
         place_scales(0)
         words.append(place([P, T], I32, "words1", WORDS1_AT))
         load_words(1)
-        w_last.append(place([P, PACK, P], F32, "w_last1", W_LAST1_AT))
-        load_w(w_last[1], 1, slice(P, N))
         place_scales(1)
 
         x_codes = []
         w_codes = {}
         w_planes = {}
+        tiles = [slice(m * P, (m + 1) * P) for m in range(N // P)]
 
-        def group_w(raw, grouped, copy):
+        def group_w(o, m, grouped, copy):
+            raw = w_raw[o][:, :, tiles[m]]
             copy(grouped[:].rearrange("p (c i) j -> p c j i", i=RUN), raw.rearrange("p j (c i) -> p c j i", i=RUN))
             return grouped
 
@@ -152,23 +142,25 @@ def tile_picked_ysplat_none_p_kernel(
             w_codes[o, m] = codes
             w_planes[o, m] = plane
 
-        def product_pass(acc, m, o, cols):
+        def codes_tile(o, m):
+            return held.tile([P, P], U32, name="w_codes%d_%d" % (o, m), align_bytes=64)
+
+        def product_pass(acc, m, o, codes, cols, stop):
             nc.tensor.matmul_mx(
                 out=acc,
                 lhsT=w_codes[o, m][:].bitcast(FP8X4),
                 lhsT_scale=w_planes[o, m][:],
-                rhs=x_codes[o][:, cols].bitcast(FP8X4),
+                rhs=codes.bitcast(FP8X4),
                 rhs_scale=x_planes[o][PLANE_START[o] : P, cols],
                 start=(o == 0),
-                stop=(o == PASSES - 1),
+                stop=stop,
             )
 
         def turn(rows, acc):
             for b in range(V_BLOCKS):
                 nc.tensor.transpose(acc[:, b * P : (b + 1) * P], rows[:, b * P : (b + 1) * P], ident[:])
 
-        def look_up(d, offset, acc):
-            op_rows = place([P, V], F32, "op_rows%d" % d, offset)
+        def look_up(d, op_rows, acc):
             scalar_copy(op_rows[:], op_t[:].indirect(pos_t[d][:]))
             turn(op_rows, acc)
             return acc[:, OP_ROW:V:P]
@@ -182,89 +174,93 @@ def tile_picked_ysplat_none_p_kernel(
         def twice(values):
             return values.unsqueeze(1).to_broadcast([P, 2, V_BLOCKS])
 
+        def row_tile(name, tag=None):
+            return held.tile([P, V], F32, name=name, tag=tag or name)
+
         chain = held.tile([P, D + 2, V_BLOCKS], F32, name="chain")
         minus_fall = chain[:, 0:D, :]
         behind1 = chain[:, D : D + 2, :]
         fall_bank = bank(0)
         turn(fall_t, fall_bank)
-        opacity_banks = [bank(1), bank(2)]
-        opacity0 = look_up(0, OP_ROWS0_AT, opacity_banks[0])
-        opacity1 = look_up(1, OP_ROWS1_AT, opacity_banks[1])
+        opacity0 = look_up(0, place([P, V], F32, "op_rows0", OP_ROWS0_AT), bank(1))
         nc.scalar.activation(
             minus_fall, fall_bank[:, 0:V].rearrange("p (b c) -> p c b", b=V_BLOCKS)[:, FALL_ROW:P, :], COPY, scale=-1.0
         )
+        opacity1 = look_up(1, row_tile("op_rows1"), bank(2))
 
-        grouped00 = held.tile([P, P, PACK], BF16, name="grouped00", align_bytes=64)
-        group_w(w_first[:, :, 0:P], grouped00, nc.vector.tensor_copy)
-        grouped01 = group_w(w_first[:, :, P:N], place([P, P, PACK], BF16, "grouped01", GROUPED01_AT), scalar_copy)
-        quantise_w(grouped00, 0, 0, held.tile([P, P], U32, name="w_codes00", align_bytes=64))
+        grouped00 = group_w(0, 0, held.tile([P, P, PACK], BF16, name="grouped00", align_bytes=64), nc.vector.tensor_copy)
+        grouped01 = group_w(0, 1, place([P, P, PACK], BF16, "grouped01", OP_ROWS0_AT), scalar_copy)
         first_w = held.tile([P, V_BLOCKS], F32, name="first_w")
         nc.vector.tensor_tensor(first_w[:], opacity0, minus_fall[:, 0, :], MULT)
+        quantise_w(grouped00, 0, 0, codes_tile(0, 0))
         behind0 = place([P, 2, V_BLOCKS], F32, "behind0", BEHIND0_AT)
         nc.vector.scalar_tensor_tensor(behind0[:], twice(first_w[:]), 1.0, minus_fall[:, 2:D, :], ADD, MULT)
         minus_a1 = held.tile([P, V_BLOCKS], F32, name="minus_a1")
         nc.vector.tensor_tensor(minus_a1[:], opacity1, minus_fall[:, 1, :], MULT)
+        quantise_w(grouped01, 0, 1, codes_tile(0, 1))
         second_w = held.tile([P, V_BLOCKS], F32, name="second_w")
         nc.vector.scalar_tensor_tensor(second_w[:], first_w[:], 1.0, minus_a1[:], ADD, MULT)
         nc.vector.scalar_tensor_tensor(behind1, twice(minus_a1[:]), 1.0, behind0[:], ADD, MULT)
-        quantise_w(grouped01, 0, 1, held.tile([P, P], U32, name="w_codes01", align_bytes=64))
-        near_banks = [bank(1), bank(2)]
-        spread(near_banks[0], [first_w])
-        spread(near_banks[1], [second_w])
-        opacity2 = look_up(2, OP_ROWS2_AT, bank(6))
-        grouped10 = group_w(w_last[0][:], place([P, P, PACK], BF16, "grouped10", GROUPED10_AT), scalar_copy)
-        opacity3 = look_up(3, W_LAST0_AT, bank(7))
+        near_bank = bank(5)
+        spread(near_bank, [first_w, second_w])
+        opacity2 = look_up(2, place([P, V], F32, "op_rows2", W_FIRST_AT), bank(3))
+        opacity3 = look_up(3, place([P, V], F32, "op_rows3", W_FIRST_AT + ROW_BYTES), bank(4))
+        near_rows = held.tile([P, 2 * V], F32, name="near_rows")
+        nc.scalar.copy(near_rows[:], near_bank[:])
 
         x_codes.append(place([P, S], U32, "x_codes0", BEHIND0_AT))
         nc.vector.tensor_copy(x_codes[0][:], words[0][:].bitcast(U32).indirect(offs_t[:]))
-        second_rows = place([P, V], F32, "second_rows", SECOND_ROWS_AT)
-        nc.scalar.copy(second_rows[:], near_banks[1][:, 0:V])
-        third = place([P, 2, V_BLOCKS], F32, "third", THIRD_AT)
+        grouped10 = group_w(1, 0, place([P, P, PACK], BF16, "grouped10", GROUPED10_AT), nc.vector.tensor_copy)
+        grouped11 = group_w(1, 1, place([P, P, PACK], BF16, "grouped11", OP_AT), scalar_copy)
+        third = held.tile([P, 2, V_BLOCKS], F32, name="third")
         nc.vector.tensor_tensor(third[:], twice(opacity2), chain[:, 2 : D + 1 : 2, :], MULT)
+        quantise_w(grouped10, 1, 0, codes_tile(1, 0))
         behind2 = held.tile([P, V_BLOCKS], F32, name="behind2")
         nc.vector.scalar_tensor_tensor(behind2[:], third[:, 0, :], 1.0, behind1[:, 1, :], ADD, MULT)
-        quantise_w(grouped10, 1, 0, place([P, P], U32, "w_codes10", CODES10_AT))
-        grouped11 = group_w(w_last[1][:], place([P, P, PACK], BF16, "grouped11", OP_AT), scalar_copy)
-        x_codes.append(place([P, S], U32, "x_codes1", GROUPED10_AT))
+        fourth = held.tile([P, V_BLOCKS], F32, name="fourth")
+        nc.vector.tensor_tensor(fourth[:], opacity3, behind2[:], MULT)
+        far_bank = bank(3)
+        spread(far_bank, [third[:, 1, :], fourth])
+        quantise_w(grouped11, 1, 1, place([P, P], U32, "w_codes11", CODES11_AT))
 
         h = [place([P, S], F32, "h0", H0_AT), held.tile([P, S], F32, name="h1")]
-        halves = [slice(0, HALF), slice(HALF, S)]
-        h0_pieces = [slice(0, HALF), slice(HALF, HALF + P), slice(HALF + P, S)]
-        h0_banks = [bank(index)[:, 0 : cols.stop - cols.start] for index, cols in zip((4, 5, 0), h0_pieces)]
-        h1_banks = [bank(index)[:, 0:HALF] for index in (6, 3)]
-        for i, cols in enumerate(h0_pieces):
-            product_pass(h0_banks[i], 0, 0, cols)
-        for i, half in enumerate(halves):
-            product_pass(h1_banks[i], 1, 0, half)
-        for i, cols in enumerate(h0_pieces):
-            nc.vector.tensor_copy(
-                x_codes[1][:, cols], words[1][:].bitcast(U32).indirect(offs_t[:, cols.start // 16 : cols.stop // 16])
-            )
-            product_pass(h0_banks[i], 0, 1, cols)
-            nc.scalar.copy(h[0][:, cols], h0_banks[i])
-        fourth = place([P, V_BLOCKS], F32, "fourth", FOURTH_AT)
-        nc.vector.tensor_tensor(fourth[:], opacity3, behind2[:], MULT)
-        quantise_w(grouped11, 1, 1, place([P, P], U32, "w_codes11", CODES11_AT))
-        first_rows = place([P, V], F32, "first_rows", OP_AT)
-        nc.vector.tensor_copy(first_rows[:], near_banks[0][:, 0:V])
-        near_rows = [first_rows, second_rows]
-        for i, half in enumerate(halves):
-            product_pass(h1_banks[i], 1, 1, half)
-            nc.scalar.copy(h[1][:, half], h1_banks[i])
-        far_bank = bank(6)
-        spread(far_bank, [third[:, 1, :], fourth])
+        quarters = [slice(i * P, (i + 1) * P) for i in range(S // P)]
+        stretches = [
+            [slice(0, HALF), quarters[2], quarters[3]],
+            [slice(0, HALF), slice(HALF, S)],
+        ]
+        h_banks = [[bank(index) for index in (0, 1, 2)], [bank(index) for index in (6, 7)]]
+        for m in range(2):
+            for acc, cols in zip(h_banks[m], stretches[m]):
+                product_pass(acc[:, 0 : cols.stop - cols.start], m, 0, x_codes[0][:, cols], cols, False)
+
+        for i, half in enumerate(stretches[1]):
+            codes = held.tile([P, HALF], U32, name="x_codes1_%d" % i, align_bytes=64)
+            for cols in quarters[2 * i : 2 * i + 2]:
+                piece = codes[:, cols.start - half.start : cols.stop - half.start]
+                nc.vector.tensor_copy(
+                    piece, words[1][:].bitcast(U32).indirect(offs_t[:, cols.start // 16 : cols.stop // 16])
+                )
+                for acc, stretch in zip(h_banks[0], stretches[0]):
+                    if stretch.start <= cols.start < stretch.stop:
+                        first = cols.start - stretch.start
+                        product_pass(acc[:, first : first + P], 0, 1, piece, cols, cols.stop == stretch.stop)
+            product_pass(h_banks[1][i][:, 0:HALF], 1, 1, codes[:], half, True)
+        nc.scalar.copy(h[0][:, stretches[0][0]], h_banks[0][0][:, 0:HALF])
+        nc.scalar.copy(h[1][:, stretches[1][0]], h_banks[1][0][:, 0:HALF])
+        for i in (1, 2):
+            nc.vector.tensor_copy(h[0][:, stretches[0][i]], h_banks[0][i][:, 0:P])
+        nc.scalar.copy(h[1][:, stretches[1][1]], h_banks[1][1][:, 0:HALF])
+
 
         def weighted(m, d, tag):
-            product = held.tile([P, V], F32, name="product%d_%d" % (m, d), tag=tag)
-            nc.vector.tensor_tensor(product[:], h[m][:].indirect(pos_t[d][:]), near_rows[d][:], MULT)
+            product = row_tile("product%d_%d" % (m, d), tag)
+            nc.vector.tensor_tensor(product[:], h[m][:].indirect(pos_t[d][:]), near_rows[:, d * V : (d + 1) * V], MULT)
             return product
 
         def picked(m, d, columns):
             scalar_copy(columns[:], h[m][:].indirect(pos_t[d][:]))
             return columns
-
-        def tagged(name, tag):
-            return held.tile([P, V], F32, name=name, tag=tag)
 
         def times(columns, m, d, cols):
             product = held.tile([P, cols.stop - cols.start], F32, name="product%d_%d_%d" % (m, d, cols.start))
@@ -277,10 +273,10 @@ def tile_picked_ysplat_none_p_kernel(
 
         whole = slice(0, V)
         blocks = [slice(b * P, (b + 1) * P) for b in range(V_BLOCKS)]
-        sum0 = bank(1)
-        sum1 = [bank(2)[:, 0:P], bank(4)[:, 0:P]]
-        total0 = bank(0)
-        total1 = [bank(3)[:, 0:P], bank(7)[:, 0:P]]
+        sum0 = bank(4)
+        sum1 = [bank(5)[:, 0:P], bank(0)[:, 0:P]]
+        total0 = bank(1)
+        total1 = [bank(2)[:, 0:P], bank(6)[:, 0:P]]
 
         def add0(product, start, stop):
             for b, cols in enumerate(blocks):
@@ -290,18 +286,18 @@ def tile_picked_ysplat_none_p_kernel(
             for b, cols in enumerate(blocks):
                 add_turned(sum1[b], product[:, cols], start, False)
 
-        add0(weighted(0, 1, "p01"), True, False)
+        add0(weighted(0, 0, "p00"), True, False)
         columns02 = picked(0, 2, place([P, V], F32, "columns0_2", CODES11_AT))
-        add0(weighted(0, 0, "p00"), False, False)
-        columns12 = picked(1, 2, tagged("columns1_2", "c12"))
-        columns13 = picked(1, 3, tagged("columns1_3", "c13"))
-        add1(weighted(1, 0, "p10"), True)
+        add0(weighted(0, 1, "p01"), False, False)
+        columns12 = picked(1, 2, row_tile("columns1_2", "c12"))
+        columns13 = picked(1, 3, row_tile("columns1_3", "c13"))
         add0(times(columns02, 0, 2, whole), False, True)
+        add1(weighted(1, 0, "p10"), True)
         add1(times(columns12, 1, 2, whole), False)
         for b, cols in enumerate(blocks):
             add_turned(sum1[b], times(columns13, 1, 3, cols)[:], False, True)
-        columns03 = picked(0, 3, tagged("columns0_3", "p10"))
-        summed0 = held.tile([P, V], F32, name="summed0")
+        columns03 = picked(0, 3, row_tile("columns0_3", "p01"))
+        summed0 = place([P, V], F32, "summed0", H0_AT)
         nc.scalar.activation(summed0[:], sum0[:, whole], COPY, scale=-1.0)
         turn(summed0, total0)
         last1 = weighted(1, 1, "c12")

@@ -28,11 +28,12 @@ GROUPED10_AT = WORDS0_AT
 WORDS1_AT = 8 * KIB
 SCALES_AT = WORDS1_AT + 4 * T - LINK
 W_FIRST_AT = 20 * KIB
-OP_AT = 24 * KIB
+OP_AT = 25 * KIB
 BEHIND0_AT = 28 * KIB
 H0_AT = 32 * KIB
 CODES11_AT = 36 * KIB
 OP_ROWS0_AT = 38 * KIB
+W_LAST_AT = 40 * KIB
 
 FLOPS = 2 * K * N * S
 
@@ -71,7 +72,7 @@ def tile_picked_ysplat_none_p_kernel(
         fall_t = held.tile([P, V], F32, name="fall_t")
         words = [place([P, T], I32, "words0", WORDS0_AT)]
         scales = place([P, T], U8, "scales", SCALES_AT)
-        w_raw = [place([P, PACK, N], F32, "w_raw0", W_FIRST_AT), held.tile([P, PACK, N], F32, name="w_raw1")]
+        w_raw = [place([P, PACK, N], F32, "w_raw0", W_FIRST_AT), place([P, PACK, N], F32, "w_raw1", W_LAST_AT)]
         ident = held.tile([P, P], F32, name="ident")
         x_rows = held.tile([P, S], U8, name="x_rows", align_bytes=64)
         x_planes = [held.tile([P, S], U8, name="x_planes%d" % o, align_bytes=64) for o in range(PASSES)]
@@ -145,14 +146,14 @@ def tile_picked_ysplat_none_p_kernel(
         def codes_tile(o, m):
             return held.tile([P, P], U32, name="w_codes%d_%d" % (o, m), align_bytes=64)
 
-        def product_pass(acc, m, o, codes, cols, stop):
+        def product_pass(acc, m, o, codes, cols, start, stop):
             nc.tensor.matmul_mx(
                 out=acc,
                 lhsT=w_codes[o, m][:].bitcast(FP8X4),
                 lhsT_scale=w_planes[o, m][:],
                 rhs=codes.bitcast(FP8X4),
                 rhs_scale=x_planes[o][PLANE_START[o] : P, cols],
-                start=(o == 0),
+                start=start,
                 stop=stop,
             )
 
@@ -161,7 +162,7 @@ def tile_picked_ysplat_none_p_kernel(
                 nc.tensor.transpose(acc[:, b * P : (b + 1) * P], rows[:, b * P : (b + 1) * P], ident[:])
 
         def look_up(d, op_rows, acc):
-            scalar_copy(op_rows[:], op_t[:].indirect(pos_t[d][:]))
+            scalar_copy(op_rows[:, 0:V], op_t[:].indirect(pos_t[d][:]))
             turn(op_rows, acc)
             return acc[:, OP_ROW:V:P]
 
@@ -182,11 +183,11 @@ def tile_picked_ysplat_none_p_kernel(
         behind1 = chain[:, D : D + 2, :]
         fall_bank = bank(0)
         turn(fall_t, fall_bank)
-        opacity0 = look_up(0, place([P, V], F32, "op_rows0", OP_ROWS0_AT), bank(1))
+        opacity0 = look_up(0, place([P, V], F32, "op_rows0", OP_ROWS0_AT), fall_bank[:, V : 2 * V])
         nc.scalar.activation(
             minus_fall, fall_bank[:, 0:V].rearrange("p (b c) -> p c b", b=V_BLOCKS)[:, FALL_ROW:P, :], COPY, scale=-1.0
         )
-        opacity1 = look_up(1, row_tile("op_rows1"), bank(2))
+        opacity1 = look_up(1, row_tile("op_rows1"), bank(1))
 
         grouped00 = group_w(0, 0, held.tile([P, P, PACK], BF16, name="grouped00", align_bytes=64), nc.vector.tensor_copy)
         grouped01 = group_w(0, 1, place([P, P, PACK], BF16, "grouped01", OP_ROWS0_AT), scalar_copy)
@@ -201,57 +202,59 @@ def tile_picked_ysplat_none_p_kernel(
         second_w = held.tile([P, V_BLOCKS], F32, name="second_w")
         nc.vector.scalar_tensor_tensor(second_w[:], first_w[:], 1.0, minus_a1[:], ADD, MULT)
         nc.vector.scalar_tensor_tensor(behind1, twice(minus_a1[:]), 1.0, behind0[:], ADD, MULT)
-        near_bank = bank(5)
+        near_bank = bank(1)
         spread(near_bank, [first_w, second_w])
-        opacity2 = look_up(2, place([P, V], F32, "op_rows2", W_FIRST_AT), bank(3))
-        opacity3 = look_up(3, place([P, V], F32, "op_rows3", W_FIRST_AT + ROW_BYTES), bank(4))
-        near_rows = held.tile([P, 2 * V], F32, name="near_rows")
-        nc.scalar.copy(near_rows[:], near_bank[:])
+        late_rows = place([P, 2 * V], F32, "late_rows", W_FIRST_AT)
+        opacity2 = look_up(2, late_rows[:, 0:V], bank(2))
+        opacity3 = look_up(3, late_rows[:, V : 2 * V], bank(3))
 
         x_codes.append(place([P, S], U32, "x_codes0", BEHIND0_AT))
         nc.vector.tensor_copy(x_codes[0][:], words[0][:].bitcast(U32).indirect(offs_t[:]))
         grouped10 = group_w(1, 0, place([P, P, PACK], BF16, "grouped10", GROUPED10_AT), nc.vector.tensor_copy)
         grouped11 = group_w(1, 1, place([P, P, PACK], BF16, "grouped11", OP_AT), scalar_copy)
+        near_rows = place([P, 2 * V], F32, "near_rows", W_LAST_AT)
+        nc.scalar.copy(near_rows[:], near_bank[:])
         third = held.tile([P, 2, V_BLOCKS], F32, name="third")
         nc.vector.tensor_tensor(third[:], twice(opacity2), chain[:, 2 : D + 1 : 2, :], MULT)
         quantise_w(grouped10, 1, 0, codes_tile(1, 0))
         behind2 = held.tile([P, V_BLOCKS], F32, name="behind2")
         nc.vector.scalar_tensor_tensor(behind2[:], third[:, 0, :], 1.0, behind1[:, 1, :], ADD, MULT)
+        quantise_w(grouped11, 1, 1, place([P, P], U32, "w_codes11", CODES11_AT))
         fourth = held.tile([P, V_BLOCKS], F32, name="fourth")
         nc.vector.tensor_tensor(fourth[:], opacity3, behind2[:], MULT)
-        far_bank = bank(3)
-        spread(far_bank, [third[:, 1, :], fourth])
-        quantise_w(grouped11, 1, 1, place([P, P], U32, "w_codes11", CODES11_AT))
 
         h = [place([P, S], F32, "h0", H0_AT), held.tile([P, S], F32, name="h1")]
         quarters = [slice(i * P, (i + 1) * P) for i in range(S // P)]
-        stretches = [
-            [slice(0, HALF), quarters[2], quarters[3]],
-            [slice(0, HALF), slice(HALF, S)],
+        stretches = [slice(0, HALF), quarters[2], quarters[3]]
+        front_bank = bank(0)
+        h_banks = [
+            [front_bank[:, m * HALF : (m + 1) * HALF]] + [bank(index)[:, 0:P] for index in (4 + 2 * m, 5 + 2 * m)]
+            for m in range(2)
         ]
-        h_banks = [[bank(index) for index in (0, 1, 2)], [bank(index) for index in (6, 7)]]
         for m in range(2):
-            for acc, cols in zip(h_banks[m], stretches[m]):
-                product_pass(acc[:, 0 : cols.stop - cols.start], m, 0, x_codes[0][:, cols], cols, False)
+            for i, cols in enumerate(stretches):
+                product_pass(h_banks[m][i], m, 0, x_codes[0][:, cols], cols, (m, i) != (1, 0), False)
 
-        for i, half in enumerate(stretches[1]):
-            codes = held.tile([P, HALF], U32, name="x_codes1_%d" % i, align_bytes=64)
-            for cols in quarters[2 * i : 2 * i + 2]:
-                piece = codes[:, cols.start - half.start : cols.stop - half.start]
-                nc.vector.tensor_copy(
-                    piece, words[1][:].bitcast(U32).indirect(offs_t[:, cols.start // 16 : cols.stop // 16])
-                )
-                for acc, stretch in zip(h_banks[0], stretches[0]):
-                    if stretch.start <= cols.start < stretch.stop:
-                        first = cols.start - stretch.start
-                        product_pass(acc[:, first : first + P], 0, 1, piece, cols, cols.stop == stretch.stop)
-            product_pass(h_banks[1][i][:, 0:HALF], 1, 1, codes[:], half, True)
-        nc.scalar.copy(h[0][:, stretches[0][0]], h_banks[0][0][:, 0:HALF])
-        nc.scalar.copy(h[1][:, stretches[1][0]], h_banks[1][0][:, 0:HALF])
+        def gather_last(codes, cols):
+            nc.vector.tensor_copy(codes, words[1][:].bitcast(U32).indirect(offs_t[:, cols.start // 16 : cols.stop // 16]))
+
+        front = held.tile([P, HALF], U32, name="x_codes1_front", align_bytes=64)
+        for i in range(2):
+            gather_last(front[:, quarters[i]], quarters[i])
+            product_pass(h_banks[0][0][:, quarters[i]], 0, 1, front[:, quarters[i]], quarters[i], False, False)
+        product_pass(h_banks[1][0], 1, 1, front[:], stretches[0], False, True)
         for i in (1, 2):
-            nc.vector.tensor_copy(h[0][:, stretches[0][i]], h_banks[0][i][:, 0:P])
-        nc.scalar.copy(h[1][:, stretches[1][1]], h_banks[1][1][:, 0:HALF])
-
+            codes = held.tile([P, P], U32, name="x_codes1_%d" % i, align_bytes=64)
+            gather_last(codes[:], stretches[i])
+            for m in range(2):
+                product_pass(h_banks[m][i], m, 1, codes[:], stretches[i], False, True)
+        for m in range(2):
+            nc.scalar.copy(h[m][:, stretches[0]], h_banks[m][0])
+        for m, i in ((0, 1), (0, 2), (1, 1)):
+            nc.vector.tensor_copy(h[m][:, stretches[i]], h_banks[m][i])
+        nc.scalar.copy(h[1][:, stretches[2]], h_banks[1][2])
+        far_bank = bank(4)
+        spread(far_bank, [third[:, 1, :], fourth])
 
         def weighted(m, d, tag):
             product = row_tile("product%d_%d" % (m, d), tag)
@@ -273,10 +276,10 @@ def tile_picked_ysplat_none_p_kernel(
 
         whole = slice(0, V)
         blocks = [slice(b * P, (b + 1) * P) for b in range(V_BLOCKS)]
-        sum0 = bank(4)
-        sum1 = [bank(5)[:, 0:P], bank(0)[:, 0:P]]
-        total0 = bank(1)
-        total1 = [bank(2)[:, 0:P], bank(6)[:, 0:P]]
+        sum0 = bank(1)
+        sum1 = [bank(3)[:, 0:P], bank(2)[:, 0:P]]
+        total0 = bank(0)
+        total1 = [bank(5)[:, 0:P], bank(6)[:, 0:P]]
 
         def add0(product, start, stop):
             for b, cols in enumerate(blocks):
@@ -300,12 +303,21 @@ def tile_picked_ysplat_none_p_kernel(
         summed0 = place([P, V], F32, "summed0", H0_AT)
         nc.scalar.activation(summed0[:], sum0[:, whole], COPY, scale=-1.0)
         turn(summed0, total0)
-        last1 = weighted(1, 1, "c12")
+        last1 = row_tile("product1_1", "c12")
+
+        def weighted_block(cols):
+            offsets = pos_t[1][:, cols.start // 16 : cols.stop // 16]
+            nc.vector.tensor_tensor(
+                last1[:, cols], h[1][:].indirect(offsets), near_rows[:, V + cols.start : V + cols.stop], MULT
+            )
+
+        weighted_block(blocks[0])
+        last0 = times(columns03, 0, 3, whole)
+        weighted_block(blocks[1])
         for b in range(V_BLOCKS):
             summed1 = held.tile([P, P], F32, name="summed1_%d" % b)
             nc.scalar.activation(summed1[:], sum1[b], COPY, scale=-1.0)
             nc.tensor.transpose(total1[b], summed1[:], ident[:])
-        last0 = times(columns03, 0, 3, whole)
         results = [(0, whole, total0[:, whole], last0)] + [(1, blocks[b], total1[b], last1) for b in range(V_BLOCKS)]
         for m, cols, total, last in results:
             result = held.tile([P, cols.stop - cols.start], F32, name="result%d_%d" % (m, cols.start))

@@ -30,7 +30,7 @@ SCALES_AT = WORDS1_AT + 4 * T - LINK
 W_FIRST_AT = 20 * KIB
 OP_AT = 25 * KIB
 BEHIND0_AT = 28 * KIB
-H0_AT = 32 * KIB
+COLUMNS12_AT = 33 * KIB
 CODES11_AT = 36 * KIB
 OP_ROWS0_AT = 38 * KIB
 W_LAST_AT = 40 * KIB
@@ -223,7 +223,7 @@ def tile_picked_ysplat_none_p_kernel(
         fourth = held.tile([P, V_BLOCKS], F32, name="fourth")
         nc.vector.tensor_tensor(fourth[:], opacity3, behind2[:], MULT)
 
-        h = [place([P, S], F32, "h0", H0_AT), held.tile([P, S], F32, name="h1")]
+        h = [held.tile([P, S], F32, name="h0"), held.tile([P, S], F32, name="h1")]
         quarters = [slice(i * P, (i + 1) * P) for i in range(S // P)]
         stretches = [slice(0, HALF), quarters[2], quarters[3]]
         front_bank = bank(0)
@@ -292,7 +292,7 @@ def tile_picked_ysplat_none_p_kernel(
         add0(weighted(0, 0, "p00"), True, False)
         columns02 = picked(0, 2, place([P, V], F32, "columns0_2", CODES11_AT))
         add0(weighted(0, 1, "p01"), False, False)
-        columns12 = picked(1, 2, row_tile("columns1_2", "c12"))
+        columns12 = picked(1, 2, place([P, V], F32, "columns1_2", COLUMNS12_AT))
         columns13 = picked(1, 3, row_tile("columns1_3", "c13"))
         add0(times(columns02, 0, 2, whole), False, True)
         add1(weighted(1, 0, "p10"), True)
@@ -300,10 +300,10 @@ def tile_picked_ysplat_none_p_kernel(
         for b, cols in enumerate(blocks):
             add_turned(sum1[b], times(columns13, 1, 3, cols)[:], False, True)
         columns03 = picked(0, 3, row_tile("columns0_3", "p01"))
-        summed0 = place([P, V], F32, "summed0", H0_AT)
-        nc.scalar.activation(summed0[:], sum0[:, whole], COPY, scale=-1.0)
+        summed0 = place([P, V], F32, "summed0", COLUMNS12_AT - ROW_BYTES // 2)
+        nc.vector.tensor_scalar(summed0[:], sum0[:, whole], -1.0, None, MULT)
         turn(summed0, total0)
-        last1 = row_tile("product1_1", "c12")
+        last1 = place([P, V], F32, "product1_1", COLUMNS12_AT + ROW_BYTES // 2)
 
         def weighted_block(cols):
             offsets = pos_t[1][:, cols.start // 16 : cols.stop // 16]

@@ -301,7 +301,7 @@ def tile_picked_ysplat_none_p_kernel(
             add_turned(sum1[b], times(columns13, 1, 3, cols)[:], False, True)
         columns03 = picked(0, 3, row_tile("columns0_3", "p01"))
         summed0 = place([P, V], F32, "summed0", COLUMNS12_AT - ROW_BYTES // 2)
-        nc.vector.tensor_scalar(summed0[:], sum0[:, whole], -1.0, None, MULT)
+        nc.scalar.activation(summed0[:], sum0[:, whole], COPY, scale=-1.0)
         turn(summed0, total0)
         last1 = place([P, V], F32, "product1_1", COLUMNS12_AT + ROW_BYTES // 2)
 

from contextlib import ExitStack

import concourse.mybir as mybir
from concourse.masks import make_identity

K, T, S, V, N, D = 1024, 2048, 512, 256, 256, 4
P = 128
QUADRANT = 32
PACK = 4
K_PASS = P * PACK
PASSES = K // K_PASS
PLANE_ROWS = K_PASS // 32
V_BLOCKS = V // P
HALF = S // 2
BANK = 512
RUN = 4

ROWS_AT = P - PASSES * PLANE_ROWS
PLANE_START = (12, 0)
OP_ROW = P - 1
FALL_ROW = P - D

KIB = 1024
LINK = 64
ROW_BYTES = 4 * V
WORDS0_AT = 0
GROUPED10_AT = WORDS0_AT
WORDS1_AT = 8 * KIB
SCALES_AT = WORDS1_AT + 4 * T - LINK
W_FIRST_AT = 20 * KIB
OP_AT = 25 * KIB
BEHIND0_AT = 28 * KIB
COLUMNS12_AT = 33 * KIB
CODES11_AT = 36 * KIB
OP_ROWS0_AT = 38 * KIB
W_LAST_AT = 40 * KIB

FLOPS = 2 * K * N * S

F32 = mybir.dt.float32
BF16 = mybir.dt.bfloat16
I32 = mybir.dt.int32
U32 = mybir.dt.uint32
U16 = mybir.dt.uint16
U8 = mybir.dt.uint8
FP8X4 = mybir.dt.float8_e4m3fn_x4
COPY = mybir.ActivationFunctionType.Copy
MULT = mybir.AluOpType.mult
ADD = mybir.AluOpType.add
SUBTRACT = mybir.AluOpType.subtract


def tile_picked_ysplat_none_p_kernel(
    tc, x_words, x_scales, w1, op, fall, offs, pos1, pos2, pos3, pos4, out
):
    nc = tc.nc
    with ExitStack() as ctx:
        held = ctx.enter_context(tc.tile_pool(name="held", bufs=1))
        placed = ctx.enter_context(tc.tile_pool(name="placed", bufs=1))
        psum = ctx.enter_context(tc.psum_pool(name="psum", bufs=1))

        def bank(index):
            return psum.tile([P, BANK], F32, name="bank%d" % index)

        def place(shape, dtype, name, offset):
            return placed.tile(shape, dtype, name=name, align_bytes=LINK, offset=offset)

        offs_t = held.tile([P, S // 16], U16, name="offs_t")
        pos_t = [held.tile([P, V // 16], U16, name="pos_t%d" % d) for d in range(D)]
        pos = [pos1, pos2, pos3, pos4]
        op_t = place([P, S], F32, "op_t", OP_AT)
        fall_t = held.tile([P, V], F32, name="fall_t")
        words = [place([P, T], I32, "words0", WORDS0_AT)]
        scales = place([P, T], U8, "scales", SCALES_AT)
        w_raw = [place([P, PACK, N], F32, "w_raw0", W_FIRST_AT), place([P, PACK, N], F32, "w_raw1", W_LAST_AT)]
        ident = held.tile([P, P], F32, name="ident")
        x_rows = held.tile([P, S], U8, name="x_rows", align_bytes=64)
        x_planes = [held.tile([P, S], U8, name="x_planes%d" % o, align_bytes=64) for o in range(PASSES)]

        nc.vector.memset(op_t[0:OP_ROW, :], 0.0)
        nc.vector.memset(scales[0:ROWS_AT, :].bitcast(I32), 0)
        make_identity(nc, ident[:])
        nc.scalar.activation(fall_t[0:FALL_ROW, :], op_t[0:FALL_ROW, 0:V], COPY)
        for o in range(PASSES):
            nc.gpsimd.memset(x_planes[o][:].bitcast(I32), 0)

        def load_words(o):
            nc.sync.dma_start(words[o][:], x_words[o].rearrange("p c r -> p (c r)").bitcast(I32))

        def load_w(o):
            rows = w1[o * K_PASS : (o + 1) * K_PASS, :]
            nc.sync.dma_start(w_raw[o][:], rows.rearrange("(p j) n -> p j n", j=PACK))

        nc.sync.dma_start(scales[ROWS_AT:P, :].bitcast(I32), x_scales.rearrange("o q c -> (o q) c").bitcast(I32))
        nc.sync.dma_start(offs_t[:], offs)
        nc.scalar.dma_start(op_t[OP_ROW:P, :], op[0:1, :])
        nc.sync.dma_start(pos_t[0][:], pos[0])
        load_w(0)
        nc.scalar.dma_start(fall_t[FALL_ROW:P, :], fall[:, 0, :])
        nc.sync.dma_start(pos_t[1][:], pos[1])
        load_words(0)
        nc.sync.dma_start(pos_t[2][:], pos[2])
        nc.sync.dma_start(pos_t[3][:], pos[3])
        load_w(1)

        nc.vector.tensor_copy(x_rows[:], scales[:].indirect(offs_t[:]))

        def place_scales(o):
            for q in range(P // QUADRANT):
                source = ROWS_AT + PLANE_ROWS * o + 4 * q
                target = QUADRANT * q + PLANE_START[o]
                if source == target:
                    rows = slice(QUADRANT * q, QUADRANT * (q + 1))
                    nc.vector.tensor_copy(x_planes[o][rows, :].bitcast(I32), x_rows[rows, :].bitcast(I32))
                else:
                    nc.sync.dma_start(
                        x_planes[o][target : target + 4, :].bitcast(I32), x_rows[source : source + 4, :].bitcast(I32)
                    )

        place_scales(0)
        words.append(place([P, T], I32, "words1", WORDS1_AT))
        load_words(1)
        place_scales(1)

        x_codes = []
        w_codes = {}
        w_planes = {}
        tiles = [slice(m * P, (m + 1) * P) for m in range(N // P)]

        def group_w(o, m, grouped, copy):
            raw = w_raw[o][:, :, tiles[m]]
            copy(grouped[:].rearrange("p (c i) j -> p c j i", i=RUN), raw.rearrange("p j (c i) -> p c j i", i=RUN))
            return grouped

        def scalar_copy(dst, src):
            nc.scalar.activation(dst, src, COPY)

        def quantise_w(grouped, o, m, codes):
            plane = held.tile([P, P], U8, name="w_planes%d_%d" % (o, m), align_bytes=64)
            nc.vector.quantize_mx(
                out=codes[:].bitcast(FP8X4), scales=plane[:], in_=grouped[:].rearrange("p n j -> p (n j)")
            )
            w_codes[o, m] = codes
            w_planes[o, m] = plane

        def codes_tile(o, m):
            return held.tile([P, P], U32, name="w_codes%d_%d" % (o, m), align_bytes=64)

        def product_pass(acc, m, o, codes, cols, start, stop):
            nc.tensor.matmul_mx(
                out=acc,
                lhsT=w_codes[o, m][:].bitcast(FP8X4),
                lhsT_scale=w_planes[o, m][:],
                rhs=codes.bitcast(FP8X4),
                rhs_scale=x_planes[o][PLANE_START[o] : P, cols],
                start=start,
                stop=stop,
            )

        def turn(rows, acc):
            for b in range(V_BLOCKS):
                nc.tensor.transpose(acc[:, b * P : (b + 1) * P], rows[:, b * P : (b + 1) * P], ident[:])

        def look_up(d, op_rows, acc):
            scalar_copy(op_rows[:, 0:V], op_t[:].indirect(pos_t[d][:]))
            turn(op_rows, acc)
            return acc[:, OP_ROW:V:P]

        def spread(acc, weights):
            for i, weight in enumerate(weights):
                for b in range(V_BLOCKS):
                    first = i * V + b * P
                    nc.tensor.transpose(acc[:, first : first + P], weight[:, b : b + 1].to_broadcast([P, P]), ident[:])

        def twice(values):
            return values.unsqueeze(1).to_broadcast([P, 2, V_BLOCKS])

        def row_tile(name, tag=None):
            return held.tile([P, V], F32, name=name, tag=tag or name)

        chain = held.tile([P, D + 2, V_BLOCKS], F32, name="chain")
        minus_fall = chain[:, 0:D, :]
        behind1 = chain[:, D : D + 2, :]
        fall_bank = bank(0)
        turn(fall_t, fall_bank)
        opacity0 = look_up(0, place([P, V], F32, "op_rows0", OP_ROWS0_AT), fall_bank[:, V : 2 * V])
        nc.scalar.activation(
            minus_fall, fall_bank[:, 0:V].rearrange("p (b c) -> p c b", b=V_BLOCKS)[:, FALL_ROW:P, :], COPY, scale=-1.0
        )
        opacity1 = look_up(1, row_tile("op_rows1"), bank(1))

        grouped00 = group_w(0, 0, held.tile([P, P, PACK], BF16, name="grouped00", align_bytes=64), nc.vector.tensor_copy)
        grouped01 = group_w(0, 1, place([P, P, PACK], BF16, "grouped01", OP_ROWS0_AT), scalar_copy)
        first_w = held.tile([P, V_BLOCKS], F32, name="first_w")
        nc.vector.tensor_tensor(first_w[:], opacity0, minus_fall[:, 0, :], MULT)
        quantise_w(grouped00, 0, 0, codes_tile(0, 0))
        behind0 = place([P, 2, V_BLOCKS], F32, "behind0", BEHIND0_AT)
        nc.vector.scalar_tensor_tensor(behind0[:], twice(first_w[:]), 1.0, minus_fall[:, 2:D, :], ADD, MULT)
        minus_a1 = held.tile([P, V_BLOCKS], F32, name="minus_a1")
        nc.vector.tensor_tensor(minus_a1[:], opacity1, minus_fall[:, 1, :], MULT)
        quantise_w(grouped01, 0, 1, codes_tile(0, 1))
        second_w = held.tile([P, V_BLOCKS], F32, name="second_w")
        nc.vector.scalar_tensor_tensor(second_w[:], first_w[:], 1.0, minus_a1[:], ADD, MULT)
        nc.vector.scalar_tensor_tensor(behind1, twice(minus_a1[:]), 1.0, behind0[:], ADD, MULT)
        near_bank = bank(1)
        spread(near_bank, [first_w, second_w])
        late_rows = place([P, 2 * V], F32, "late_rows", W_FIRST_AT)
        opacity2 = look_up(2, late_rows[:, 0:V], bank(2))
        opacity3 = look_up(3, late_rows[:, V : 2 * V], bank(3))

        x_codes.append(place([P, S], U32, "x_codes0", BEHIND0_AT))
        nc.vector.tensor_copy(x_codes[0][:], words[0][:].bitcast(U32).indirect(offs_t[:]))
        grouped10 = group_w(1, 0, place([P, P, PACK], BF16, "grouped10", GROUPED10_AT), nc.vector.tensor_copy)
        grouped11 = group_w(1, 1, place([P, P, PACK], BF16, "grouped11", OP_AT), scalar_copy)
        near_rows = place([P, 2 * V], F32, "near_rows", W_LAST_AT)
        nc.scalar.copy(near_rows[:], near_bank[:])
        third = held.tile([P, 2, V_BLOCKS], F32, name="third")
        nc.vector.tensor_tensor(third[:], twice(opacity2), chain[:, 2 : D + 1 : 2, :], MULT)
        quantise_w(grouped10, 1, 0, codes_tile(1, 0))
        behind2 = held.tile([P, V_BLOCKS], F32, name="behind2")
        nc.vector.scalar_tensor_tensor(behind2[:], third[:, 0, :], 1.0, behind1[:, 1, :], ADD, MULT)
        quantise_w(grouped11, 1, 1, place([P, P], U32, "w_codes11", CODES11_AT))
        fourth = held.tile([P, V_BLOCKS], F32, name="fourth")
        nc.vector.tensor_tensor(fourth[:], opacity3, behind2[:], MULT)

        h = [held.tile([P, S], F32, name="h0"), held.tile([P, S], F32, name="h1")]
        quarters = [slice(i * P, (i + 1) * P) for i in range(S // P)]
        stretches = [slice(0, HALF), quarters[2], quarters[3]]
        front_bank = bank(0)
        h_banks = [
            [front_bank[:, m * HALF : (m + 1) * HALF]] + [bank(index)[:, 0:P] for index in (4 + 2 * m, 5 + 2 * m)]
            for m in range(2)
        ]
        for m in range(2):
            for i, cols in enumerate(stretches):
                product_pass(h_banks[m][i], m, 0, x_codes[0][:, cols], cols, (m, i) != (1, 0), False)

        def gather_last(codes, cols):
            nc.vector.tensor_copy(codes, words[1][:].bitcast(U32).indirect(offs_t[:, cols.start // 16 : cols.stop // 16]))

        front = held.tile([P, HALF], U32, name="x_codes1_front", align_bytes=64)
        for i in range(2):
            gather_last(front[:, quarters[i]], quarters[i])
            product_pass(h_banks[0][0][:, quarters[i]], 0, 1, front[:, quarters[i]], quarters[i], False, False)
        product_pass(h_banks[1][0], 1, 1, front[:], stretches[0], False, True)
        for i in (1, 2):
            codes = held.tile([P, P], U32, name="x_codes1_%d" % i, align_bytes=64)
            gather_last(codes[:], stretches[i])
            for m in range(2):
                product_pass(h_banks[m][i], m, 1, codes[:], stretches[i], False, True)
        for m in range(2):
            nc.scalar.copy(h[m][:, stretches[0]], h_banks[m][0])
        for m, i in ((0, 1), (0, 2), (1, 1)):
            nc.vector.tensor_copy(h[m][:, stretches[i]], h_banks[m][i])
        nc.scalar.copy(h[1][:, stretches[2]], h_banks[1][2])
        far_bank = bank(4)
        spread(far_bank, [third[:, 1, :], fourth])

        def weighted(m, d, tag):
            product = row_tile("product%d_%d" % (m, d), tag)
            nc.vector.tensor_tensor(product[:], h[m][:].indirect(pos_t[d][:]), near_rows[:, d * V : (d + 1) * V], MULT)
            return product

        def picked(m, d, columns):
            scalar_copy(columns[:], h[m][:].indirect(pos_t[d][:]))
            return columns

        def times(columns, m, d, cols):
            product = held.tile([P, cols.stop - cols.start], F32, name="product%d_%d_%d" % (m, d, cols.start))
            first = (d - 2) * V
            nc.vector.tensor_tensor(product[:], columns[:, cols], far_bank[:, first + cols.start : first + cols.stop], MULT)
            return product

        def add_turned(acc, block, start, stop):
            nc.tensor.matmul(acc, block, ident[:], is_transpose=True, start=start, stop=stop)

        whole = slice(0, V)
        blocks = [slice(b * P, (b + 1) * P) for b in range(V_BLOCKS)]
        sum0 = bank(1)
        sum1 = [bank(3)[:, 0:P], bank(2)[:, 0:P]]
        total0 = bank(0)
        total1 = [bank(5)[:, 0:P], bank(6)[:, 0:P]]

        def add0(product, start, stop):
            for b, cols in enumerate(blocks):
                add_turned(sum0[:, cols], product[:, cols], start and b == 0, stop and b == V_BLOCKS - 1)

        def add1(product, start):
            for b, cols in enumerate(blocks):
                add_turned(sum1[b], product[:, cols], start, False)

        add0(weighted(0, 0, "p00"), True, False)
        columns02 = picked(0, 2, place([P, V], F32, "columns0_2", CODES11_AT))
        add0(weighted(0, 1, "p01"), False, False)
        columns12 = picked(1, 2, place([P, V], F32, "columns1_2", COLUMNS12_AT))
        columns13 = picked(1, 3, row_tile("columns1_3", "c13"))
        add0(times(columns02, 0, 2, whole), False, True)
        add1(weighted(1, 0, "p10"), True)
        add1(times(columns12, 1, 2, whole), False)
        for b, cols in enumerate(blocks):
            add_turned(sum1[b], times(columns13, 1, 3, cols)[:], False, True)
        columns03 = picked(0, 3, row_tile("columns0_3", "p01"))
        summed0 = place([P, V], F32, "summed0", COLUMNS12_AT - ROW_BYTES // 2)
        nc.scalar.activation(summed0[:], sum0[:, whole], COPY, scale=-1.0)
        turn(summed0, total0)
        last1 = place([P, V], F32, "product1_1", COLUMNS12_AT + ROW_BYTES // 2)

        def weighted_block(cols):
            offsets = pos_t[1][:, cols.start // 16 : cols.stop // 16]
            nc.vector.tensor_tensor(
                last1[:, cols], h[1][:].indirect(offsets), near_rows[:, V + cols.start : V + cols.stop], MULT
            )

        weighted_block(blocks[0])
        last0 = times(columns03, 0, 3, whole)
        weighted_block(blocks[1])
        for b in range(V_BLOCKS):
            summed1 = held.tile([P, P], F32, name="summed1_%d" % b)
            nc.scalar.activation(summed1[:], sum1[b], COPY, scale=-1.0)
            nc.tensor.transpose(total1[b], summed1[:], ident[:])
        results = [(0, whole, total0[:, whole], last0)] + [(1, blocks[b], total1[b], last1) for b in range(V_BLOCKS)]
        for m, cols, total, last in results:
            result = held.tile([P, cols.stop - cols.start], F32, name="result%d_%d" % (m, cols.start))
            nc.vector.tensor_tensor(result[:], total, last[:, cols], SUBTRACT)
            nc.sync.dma_start(out[m * P : (m + 1) * P, cols], result[:])
